import numpy as np, ml_dtypes
CORES = [1,5,17,21,33,37,49,53]
N = 8
import mx_ref
BF = ml_dtypes.bfloat16
def gentries(a):
    return np.ascontiguousarray(a.reshape(8, 16, -1).transpose(0, 2, 1)).reshape(8, -1)
def gtable(e):
    e = np.asarray(e); return np.ascontiguousarray(e.reshape(8, -1, 16).transpose(0, 2, 1)).reshape(128, -1).astype(np.int32)
def gcols(t, e):
    v = np.concatenate([t.reshape(8, 16, -1, 4), np.zeros((8, 16, 1, 4), BF)], axis=2)
    return np.ascontiguousarray(np.stack([v[g][:, e[g]] for g in range(8)])).reshape(128, -1)
def tile(rs):
    return np.stack(rs, axis=2).reshape(128, -1).astype(BF)
def pick(q, e):
    c = np.concatenate([q[0].reshape(128, -1, 4), np.zeros((128, 1, 4), np.uint8)], axis=1); s = np.concatenate([q[1], np.ones((16, 1), np.uint8)], axis=1)
    return (np.ascontiguousarray(c[:, e].reshape(128, -1)), np.ascontiguousarray(s[:, e]))
def join(*qs):
    return (np.concatenate([q[0] for q in qs], axis=1), np.concatenate([q[1] for q in qs], axis=1))
def put(q, e, v):
    c, s = q[0].reshape(128, -1, 4).copy(), q[1].copy(); c[:, e] = v[0].reshape(128, -1, 4); s[:, e] = v[1]
    return (c.reshape(128, -1), s)
def pk(c, s):
    return (np.ascontiguousarray(c), mx_ref.live(s))
def emit(q):
    return q[0], q[1]
def packed(v, rng):
    q = [mx_ref.quantize(np.ascontiguousarray(v[r])) for r in range(N)]
    return np.stack([a for a, b in q]), np.stack([mx_ref.plane(b, rng) for a, b in q])
def values_of_codes():
    e, c = np.zeros((128, 128, 4), np.float32), np.zeros((128, 2, 4), np.uint8)
    e[np.arange(128), np.arange(128), 0] = 1
    c[:127, :, 0] = np.arange(256).reshape(2, 128).T[:127]
    return mx_ref.matmul(mx_ref.quantize(e.reshape(128, 512).astype(BF)), (c.reshape(128, 8), np.full((16, 2), 127, np.uint8))).T.reshape(-1).astype(np.float64)
CODE_VALUE, SCALE_VALUE = values_of_codes(), 2.0 ** (np.arange(256) - 127.0)
def decode(q):
    return (CODE_VALUE[q[0]].reshape(16, 8, -1, 4) * SCALE_VALUE[q[1]][:, None, :, None] + 0.0).reshape(128, -1).astype(np.float32)
def f(rng, *shape):
    return mx_ref.flush((rng.standard_normal(shape, dtype=np.float32) * np.exp2(rng.integers(-2, 3, shape[:-1] + (1,)))).astype(BF))
def wide(rng, *shape, cols=0):
    v = rng.standard_normal(shape, dtype=np.float32) * np.exp2(rng.integers(-12, 13, shape)).astype(np.float32)
    if cols: v *= np.repeat(np.exp2(rng.integers(-cols, cols + 1, shape[:-2] + (1, shape[-1] // 4))) * (rng.random(shape[:-2] + (1, shape[-1] // 4)) > 0.0625), 4, axis=-1).astype(np.float32)
    return mx_ref.flush(v.astype(BF))
C, E, B, R = 256, 16, 96, 2
L = C + B
M = L - 2 * E - 15
S = np.arange(16)
AT = np.arange(0, E, E // 4)
G = np.arange(8)[:, None, None]
def choose(s, b):
    p, n = b.copy(), b.copy()
    for k in range(1, 16):
        n[:, k] = p[:, k - 1] + E
        c = b[:, k:k + 1] + S
        d = np.max(np.abs(s[G, n[:, k, None, None] + AT] - s[G, c[:, :, None] + AT]), axis=2)
        d[c == n[:, k:k + 1]] = np.inf
        p[:, k] = b[:, k] + np.argmin(d, axis=1)
    return p, n
def places(e):
    return (e[:, :, None] + np.arange(E)).reshape(8, C)
def big(v):
    v = v.astype(np.float32)
    v[np.abs(v) < np.float32(2.0 ** -16)] = 0
    return v.astype(BF)
def numbers_of(rng):
    return {"x": big(f(rng, N, 128, 4 * C)), "u": np.array(f(rng, N, 128, 512)), "v": np.array(f(rng, N, 128, 512))}
def lists_of(rng):
    hop = rng.integers(E - E // 4, E + E // 4 + 1, (N, 8, R, 1))
    return (hop * S + rng.integers(0, M - 15 * (E + E // 4) + 1, (N, 8, R, 16))).reshape(N, 8, 16 * R)
def even(rng, k):
    return (rng.integers(0, M - 15 * E + 1, (k, R, 1)) + E * S).reshape(k, 16 * R)
def halves(rng, k):
    return rng.integers(0, C // 2 - 15 - 2 * E + 1, (k, 16)) + C // 2 * (S % 2)
def stored(l):
    return np.stack([gtable(e) for e in l])
def weights(rng, w):
    c, p = packed(w, rng)
    return {"wc": c, "ws": p}
def layers(rng):
    return weights(rng, f(rng, N, 128, 2048))
def unit(rng, a):
    w = np.zeros((N, 128, 4, 128, 4), np.float32)
    i = np.arange(128)
    for b in range(4): w[:, i, b, i, b] = a
    return weights(rng, w.reshape(N, 128, 2048).astype(BF))
def setup_inputs(rng):
    return {**numbers_of(rng), "st": stored(lists_of(rng)), **layers(rng)}
def setup_inputs_ties(rng):
    d, l = numbers_of(rng), lists_of(rng)
    o = rng.permutation(N)
    x = d["x"].reshape(N, 8, 16, C, 4)
    for r in range(N):
        k = np.zeros(C, int) if r == o[0] else rng.permutation(C) % 3
        a = x[r][:, :8, :3].copy()
        a[:, :, 2] = 0
        x[r][:, :8] = a[:, :, k]
    x[o[1]] = 0
    l[o[0], :2] = even(rng, 2)
    l[o[1], 0] = rng.integers(C, M + 1, 16 * R)
    u = d["u"].reshape(N, 8, 16, 128, 4)
    u[:, :, 8:, ::16] = 0
    return {"x": x.reshape(N, 128, 4 * C), "u": u.reshape(N, 128, 512), "v": d["v"], "st": stored(l), **layers(rng)}
def setup_inputs_near(rng):
    d, l = numbers_of(rng), lists_of(rng)
    o = rng.permutation(N)
    h, j = C // 2, np.arange(C)
    sign, t, tiny = np.ones((N, 8, C)), np.zeros((N, C), int), []
    for r in range(N):
        t[r] = np.where(j < h, h - 1 - j, j - h) if o[r] % 4 < 2 else rng.integers(0, 256, C)
        far = rng.permutation(8) % 2 == 1
        sign[r] = np.where(far[:, None] & (j >= h), -1.0, 1.0)
        l[r, far, :16] = halves(rng, 4)
        if o[r] % 4 == 1:
            e = rng.permutation(np.flatnonzero(~far))[:2]
            l[r, e, :16] = halves(rng, 2)
            tiny += [(r, int(i)) for i in e]
    g = ((t[:, :, None] >> np.arange(8)) & 1) * np.exp2(np.arange(8) - 23.0)
    x = d["x"].astype(np.float32).reshape(N, 8, 16, C, 4)
    x[:, :, 0] = 0
    x[:, :, 0, :, 0] = sign
    x[:, :, 8] = g[:, None, :, :4]
    x[:, :, 9] = g[:, None, :, 4:]
    x[:, :, 10:] = rng.integers(4, 8, (N, 8, 6, C, 4)) * rng.choice([-1.0, 1.0], (N, 8, 6, C, 4)) * 2.0 ** -20
    x *= np.where(o % 2, 2.0 ** -4, 1.0).astype(np.float32)[:, None, None, None, None]
    u = d["u"].reshape(N, 128, 128, 4)
    k = np.where(o % 2, 2.0 ** -30, 1.0).astype(np.float32).astype(BF)
    u[:, :, ::16] = 0
    for i in range(0, 128, 16):
        u[:, i, i, 0] = k
        u[:, i + 8:i + 10, i] = k[:, None, None]
    for r, i in tiny:
        w = t[r] // 8 + 32 * (j < h)
        x[r, i, :8] = 0
        x[r, i, 1, :, 0] = (8 + w % 8) * 2.0 ** -32
        x[r, i, 2, :, 0] = (8 + w % 8) * 2.0 ** -32
        x[r, i, 3, :, 0] = (8 + w // 8) * 2.0 ** -32
        u[r, :, 16 * i] = 0
        u[r, 16 * i + 1:16 * i + 4, 16 * i, 0] = (np.array([-1.0, 1.125, 1.0]) * 2.0 ** -30).astype(np.float32).astype(BF)
    return {"x": x.reshape(N, 128, 4 * C).astype(BF), "u": u.reshape(N, 128, 512), "v": d["v"], "st": stored(l), **unit(rng, 32)}
def setup_inputs_huge(rng):
    d, l = numbers_of(rng), lists_of(rng)
    o = rng.permutation(N)
    a = np.zeros((N, C))
    m = 0.9 + 0.1 * rng.random((N, 128, C, 4))
    k = 0.9 + 0.1 * rng.random((N, 128, 8, 4))
    for r in range(N):
        if o[r] % 2:
            l[r, :, :16] = even(rng, 8)[:, :16]
            if o[r] % 4 == 1:
                i = int(l[r, 0, 1])
                a[r] = rng.choice([-1.0, 1.0], C)
                a[r, i] = 1
                a[r, i + 1:i + 16] = -1
                m[r, :, i:i + 16] = 1
                k[r] = 1
            else:
                a[r] = rng.uniform(-1, 1, C)
        else:
            a[r] = np.where(np.arange(C) < C // 2, 1.0, -1.0)
            l[r, :, :16] = halves(rng, 8)
    x = 2.0 ** 30 * m * a[:, None, :, None]
    g = np.stack([rng.permutation(8) % 2 * 2.0 - 1.0 for r in range(N)])
    u = d["u"].reshape(N, 128, 128, 4)
    u[:, :, ::16] = (2.0 ** 30 * k * g[:, None, :, None]).astype(np.float32).astype(BF)
    return {"x": x.astype(np.float32).reshape(N, 128, 4 * C).astype(BF), "u": u.reshape(N, 128, 512), "v": d["v"], "st": stored(l), **unit(rng, -16)}
def setup_inputs_lists(rng):
    d, l = numbers_of(rng), lists_of(rng)
    for r in range(N):
        g = rng.permutation(8)
        l[r, g[:2]] = rng.integers(0, M + 1, (2, 16 * R))
        l[r, g[2:4]] = M
        l[r, g[4]] = np.sort(rng.integers(0, M + 1, (R, 16)), axis=1)[:, ::-1].reshape(-1)
        l[r, g[5]] = even(rng, 1)[0]
        l[r, g[6]] = rng.integers(C, M + 1, 16 * R)
        l[r, g[7]] = 0
    return {**d, "st": stored(l), **layers(rng)}
def setup_inputs_spread(rng):
    d = setup_inputs(rng)
    d["x"] = big(wide(rng, N, 128, 4 * C, cols=6))
    return d
def check_inputs(d):
    b = []
    for k in ("x", "u", "v"):
        a = np.abs(d[k].astype(np.float32))
        if not (np.isfinite(a).all() and ((a == 0) | (a >= 2.0 ** -30) & (a <= 2.0 ** 30)).all()): b.append("a value of " + k)
    if ((d["st"] < 0) | (d["st"] > M)).any(): b.append("an entry of st")
    return b
def reference(x, u, v, st, wc, ws):
    qu = [mx_ref.quantize(u[r]) for r in range(N)]
    lay = [pk(wc[r], ws[r]) for r in range(N)]
    first = [gentries(st[r]).astype(np.int64) for r in range(N)]
    now = [x[r] for r in range(N)]
    y, ol = np.zeros((N, 128, C), np.float32), np.zeros((N, 8, 16 * R), np.float32)
    oc, osc = np.zeros((N, 128, 4 * C), np.uint8), np.zeros((N, 16, C), np.uint8)
    for t in range(R):
        q = [mx_ref.quantize(now[r]) for r in range(N)]
        now = []
        for r in range(N):
            window = join(q[r], pick(q[(r + 1) % N], np.arange(B)))
            p, n = choose(mx_ref.matmul(qu[r], window)[::16], first[r][:, 16 * t:16 * t + 16])
            ol[r, :, 16 * t:16 * t + 16] = p
            d = decode(window).astype(BF)
            z = (gcols(d, places(n)).astype(np.float32) + gcols(d, places(p)).astype(np.float32)) * np.float32(0.5)
            qz = mx_ref.quantize(z.astype(BF))
            w = lay[(r + 1 + t) % N]
            h = tile([mx_ref.matmul(pick(w, np.arange(128 * b, 128 * b + 128)), qz) * np.float32(0.03125) for b in range(4)])
            now.append((decode(qz) + decode(mx_ref.quantize(h))).astype(BF))
    for r in range(N):
        q = mx_ref.quantize(now[r])
        y[r] = mx_ref.matmul(mx_ref.quantize(v[r]), q)
        oc[r], osc[r] = emit(q)
    return {"y": y, "ol": ol, "oc": oc, "osc": osc}

@@ -1,0 +1,461 @@
+from concourse.mybir import dt, AluOpType, ActivationFunctionType
+
+ALU = AluOpType
+ACT = ActivationFunctionType
+C, B, L, R = 256, 96, 352, 2
+Q4, U8, F32, BF, I32, U16 = "float8_e4m3fn_x4", "uint8", "float32", "bfloat16", "int32", "uint16"
+
+SCRATCH = {
+    "ps": ("psum", [128, 4096], F32),
+    "xb": ("sbuf", [128, 4 * C], BF), "ub": ("sbuf", [128, 512], BF), "vb": ("sbuf", [128, 512], BF),
+    "sti": ("sbuf", [128, 2], I32), "stf": ("sbuf", [128, 2], F32),
+    "uq": ("sbuf", [128, 128], Q4), "us": ("sbuf", [128, 128], U8),
+    "u2q": ("sbuf", [128, 256], Q4), "u2s": ("sbuf", [128, 256], U8),
+    "vq": ("sbuf", [128, 128], Q4), "vs": ("sbuf", [128, 128], U8),
+    "woq": ("sbuf", [128, 512], Q4), "wos": ("sbuf", [128, 512], U8),
+    "ei": ("sbuf", [128, 128], BF), "ea": ("sbuf", [128, 128], BF), "et": ("sbuf", [128, 2048], BF),
+    "eq": ("sbuf", [128, 512], Q4), "es": ("sbuf", [128, 512], U8),
+    "pti": ("sbuf", [128, 192], F32), "pt": ("sbuf", [128, 192], F32),
+    "i4": ("sbuf", [128, 8], F32), "i16": ("sbuf", [128, 16], F32),
+    "q4": ("sbuf", [128, 64], F32), "q4t": ("sbuf", [128, 64], F32),
+    "lf": ("sbuf", [128, 36], F32), "lu": ("sbuf", [128, 36], U16),
+    "upf": ("sbuf", [128, 16], I32), "upu": ("sbuf", [128, 16], U16),
+    "e4": ("sbuf", [128, 128], F32), "ci": ("sbuf", [128, 128], F32),
+    "bi": ("sbuf", [128, 64], F32), "b2": ("sbuf", [128, 64], F32),
+    "b2i": ("sbuf", [128, 64], F32), "db": ("sbuf", [128, 64], F32),
+    "a0": ("sbuf", [128, 1024], BF), "rt": ("sbuf", [128, 128], F32), "d1": ("sbuf", [128, 128], BF),
+    "pos": ("sbuf", [128, 32], F32), "yb": ("sbuf", [128, C], F32),
+    "xq2": ("sbuf", [128, C], Q4), "xs2": ("sbuf", [128, C], U8),
+}
+for _t in range(R):
+    for _n, _w, _d in (("xq", L, Q4), ("xs", L, U8), ("wq", 512, Q4), ("wp", 512, U8), ("w2", 2 * L, F32),
+                       ("otf", 128, F32), ("otc", 128, U16), ("kk", 64, F32), ("of0", 4, U16), ("pen", 256, BF),
+                       ("tg", 1024, F32), ("tb", 1024, F32), ("dd", 1024, F32), ("ab", 1024, F32),
+                       ("ms", 1028, F32), ("mb", 256, F32), ("nf", 256, BF), ("cn", 256, BF), ("fb", 256, F32),
+                       ("ft", 256, F32), ("sx", 256, U16), ("cf", 64, F32), ("po", 64, F32), ("off", 64, U16),
+                       ("dv", 4 * L, F32), ("nn", 1024, F32), ("zt", 1024, BF), ("zq", C, Q4), ("zs", C, U8),
+                       ("ht", 1024, BF), ("hq", C, Q4), ("hs", C, U8), ("xt", 1024, BF)):
+        SCRATCH["%s%d" % (_n, _t)] = ("sbuf", [128, _w], _d)
+NPOOL = 120
+SEMAPHORES = ["s%d" % _i for _i in range(NPOOL)] + ["sent", "xarr0", "xarr1", "warr0", "warr1"]
+
+STAGES = (((0, 4), (4, 8), (8, 12), (12, 16)),) * 2
+ORDER = """
+0s 1s 32v 2s 3s 18g 13g 4s 35v 1ag 15g 31v 12g 27v 28v 37v 14g 11g 17g 16g 30v 36v 1bg 7v 3ev 9g 3av 20v 3ca 33v 23v ag
+3fv 40a 3bv 24a 1fg 8v 41v 46p 19g 44p 1cg 21a 22v 29a 5s 6s 42a 25v 1dg 26v 43v 4av 2aa 1eg 48v 2da 2ca 49v 45a 4cv 2ba
+2fv 47a 34a 2ev bg cg 4bv 50p 52p 51a 54p 53a dg 4da 4ev 58p eg 62v 5da 56p 5ap 63v 7fa 5ev 84a 64v 65a 5fv 66a 85v 60a
+61a 80v 57a 67v 5ba 86v 68v 88a 81v 4fa 87a 69v 83a 82a 6av 89v 6ba 6cv 59a 55a 8av 5ca 6dv 6ev 8bv 6fv 8cv 70v 8da 74v
+71v 75v 72v 76v 73v 7aa 8ev 77v 8fv 78v 90v 79v 91v 7ca 7bv 7dv 92v 7ev 93v a3p 97v a5p 94v a4a a9p 98v a7p a6a 95v acp
+aav afp 99v a8a b5p abv 9da b2p 96v b0p 9av b3p adp b1v b6p 9bv b4a aev b7a 9cv a2a b8v 9fa 9ev bbp bca a0v a1v 3dv bdg
+beg c1p c2a bfg c3p ddv c7p c5p c4a cap c8v c6a c0g 39v cdp 38v dea d3p c9v d0p d7v d1p d2a cep dbv cbp d4p cfa d5v b9p
+cca dca d6v d9v e0p d8v e2p dav e1a eap e3v baa f2a edv e6p e4p 114a eev f3v 10fa efv f4v f0a 110v e8p f1a f5a f6a 115v
+f7v e9a e5a eba 116v f8v 118a 117a 111v f9v 113a 112a fav 119v fba e7a fcv 11av eca fdv 11bv fev 11cv ffv 100v 11da 104v
+101v 11ev 102v 105v 103v 106v 11fv 10aa 107v 120v 108v 121v 109v 122v 10ca 10bv 123v 127v 124v 128v 125v 129v 126v 12da
+10dv 12av 10ev 12bv 134p 12ev 138p 135a 136p 13ap 137a 12cv 139v 12fa 143p 13bv 132a 164s 13dp 13cv 146p 140p 141p 130v
+13ep 147p 13fa 131v 148a 144p 145v 142a 152p 14ep 153a 14cp 149v 165s 14fa 150p 15ep 151a 158p 14dv 154v 155p 15bp 15cp
+159p 15dv 15fp 156p 15aa 160a 157v 161v 16aa 169s 14ap 162p 14bv 167a 16ca 166s 163v 16ba 168s
+"""
+HUGE, PEN = 2.0 ** 92, 2.0 ** 88
+
+
+def span(v):
+    n, a, b, s = v
+    if n == "ps":
+        a, b, s = a // 512, a // 512 + 1, 1
+    m = 0
+    if s == 1:
+        return ((1 << (b - a)) - 1) << a
+    for j in range(a, b, s):
+        m |= 1 << j
+    return m
+
+
+def program(g, T, peers):
+    ops = []
+
+    def V(n, a, b, s=1):
+        return (n, a, b, s)
+
+    def ap(v):
+        n, a, b, s = v
+        return T[n][:, a:b] if s == 1 else T[n][:, a:b:s]
+
+    def width(v):
+        return len(range(v[1], v[2], v[3]))
+
+    def op(name, alts, rd, wr, acc=None, after=(), ext=None, kind="c"):
+        ops.append({"name": name, "alts": alts, "rd": rd, "wr": wr, "acc": acc, "after": list(after), "ext": ext,
+                    "kind": kind})
+
+    def vec(name, fn, cost, rd, wr):
+        op(name, {"v": (fn, cost)}, rd, wr)
+
+    def sc(x):
+        return ap(x) if isinstance(x, tuple) else x
+
+    def aps(*xs):
+        return [x for x in xs if isinstance(x, tuple)]
+
+    def memset(name, o, val, half=False):
+        vec(name, lambda: g.vector.memset(ap(o), val), ("n", width(o) * (0.5 if half else 1)), [], [o])
+
+    def copy(name, o, i):
+        vec(name, lambda: g.vector.tensor_copy(ap(o), ap(i)), ("n", width(o)), [i], [o])
+
+    def tt(name, o, a, b, alu):
+        vec(name, lambda: g.vector.tensor_tensor(ap(o), ap(a), ap(b), alu), ("n", 2 * width(o)), [a, b], [o])
+
+    def gtt(name, o, win, off, b, alu):
+        vec(name, lambda: g.vector.tensor_tensor(ap(o), ap(win).indirect(ap(off)), ap(b), alu), ("gv", width(o)),
+            [win, off, b], [o])
+
+    def gather(name, o, win, off, queues="v"):
+        alts = {}
+        if "v" in queues:
+            alts["v"] = (lambda: g.vector.tensor_copy(ap(o), ap(win).indirect(ap(off))), ("gv", width(o)))
+        if "a" in queues:
+            alts["a"] = (lambda: g.scalar.activation(ap(o), ap(win).indirect(ap(off)), ACT.Copy), ("ga", width(o)))
+        op(name, alts, [win, off], [o])
+
+    def scale(name, o, i, k, queues="va"):
+        alts = {}
+        if "v" in queues:
+            if k == 1.0:
+                alts["v"] = (lambda: g.vector.tensor_copy(ap(o), ap(i)), ("n", width(o)))
+            else:
+                alts["v"] = (lambda: g.vector.tensor_scalar(ap(o), ap(i), k, None, ALU.mult), ("n", width(o)))
+        if "a" in queues:
+            alts["a"] = (lambda: g.scalar.activation(ap(o), ap(i), ACT.Copy, scale=k), ("n", width(o)))
+        psum = [i] if i[0] == "ps" else []
+        op(name, alts, [] if psum else [i], [o] + psum)
+
+    def lin(name, o, i, k, bias, queues="va", func=None, off=None):
+        src = (lambda: ap(i)) if off is None else (lambda: ap(i).indirect(ap(off)))
+        alts = {}
+        if "v" in queues:
+            alts["v"] = (lambda: g.vector.tensor_scalar(ap(o), src(), k, sc(bias), ALU.mult, ALU.add),
+                         ("n" if off is None else "gv", width(o)))
+        if "a" in queues:
+            alts["a"] = (lambda: g.scalar.activation(ap(o), src(), func or ACT.Identity, bias=sc(bias), scale=k),
+                         ("n" if off is None else "ga", width(o)))
+        op(name, alts, [i] + aps(bias, off), [o])
+
+    def scan(name, o, d0, d1, op0, op1, f=1.0):
+        vec(name, lambda: g.vector.tensor_tensor_scan(ap(o), ap(d0), ap(d1), 0.0, op0, op1), ("n", width(o) * f),
+            [d0, d1], [o])
+
+    def transpose(name, o, i):
+        vec(name, lambda: g.vector.transpose(ap(o), ap(i)), ("n", width(o)), [i], [o])
+
+    def quant(name, q, s, a, b, i):
+        o, p = V(q, a, b), V(s, a, b)
+        vec(name, lambda: g.vector.quantize_mx(ap(o), ap(p), ap(i)), ("q", width(i)), [i], [o, p])
+
+    def mm(name, bank, lq, ls, la, rq, rs, ra, rb, start=True, stop=True, acc=None):
+        o = V("ps", 512 * bank, 512 * bank + rb - ra)
+        a, b, c, d = V(lq, la, la + 128), V(ls, la, la + 128), V(rq, ra, rb), V(rs, ra, rb)
+        op(name, {"p": (lambda: g.tensor.matmul_mx(ap(o), ap(a), ap(b), ap(c), ap(d), start, stop), ("mm", rb - ra))},
+           [a, b, c, d], [o], acc=acc)
+
+    def iota(name, o, pattern, base, cm):
+        if SCRATCH[o[0]][2] == I32:
+            fn = lambda: g.iota(ap(o), pattern, base, cm)
+        else:
+            fn = lambda: g.iota(ap(o), pattern, base, cm, allow_small_or_imprecise_dtypes=True)
+        op(name, {"g": (fn, ("io", width(o)))}, [], [o])
+
+    def dma(name, queues, dst, src, kb, rd, wr, after=()):
+        alts = {}
+        if "s" in queues:
+            alts["s"] = (lambda: g.sync.dma_start(dst(), src()), ("dma", kb))
+        if "a" in queues:
+            alts["a"] = (lambda: g.scalar.dma_start(dst(), src()), ("dma", kb))
+        op(name, alts, rd, wr, after=after, kind="dma")
+
+    def codes(v):
+        return ap(v).bitcast(dt.uint8)
+
+    last_remote = []
+
+    def ship(name, peer, sem, dq, ds, da, sq, ss, sa, n):
+        a, b, c, d = V(dq, da, da + n), V(sq, sa, sa + n), V(ds, da, da + n), V(ss, sa, sa + n)
+        kind = "none" if peer is None else "rem"
+        op(name + "c", {"g": (lambda: g.remote_dma(codes(a), codes(b), T.sem[sem], T.sem["sent"], peer[1], peer[0], peer[2]),
+                              ("rem", n / 2.0))}, [b], [], after=last_remote[-1:], kind=kind)
+        op(name + "s", {"g": (lambda: g.remote_dma(ap(c), ap(d), T.sem[sem], T.sem["sent"], peer[1], peer[0], peer[2]),
+                              ("rem", n / 8.0))}, [d], [], after=[name + "c"], kind=kind)
+        ops[-1]["eng"] = ops[-2]["eng"] = 0 if peer is None else peer[3]
+        last_remote.append(name + "s")
+
+    def arrive(name, sem, count, wr, like):
+        op(name, {"x": (None, ("arr", like))}, [], wr, ext=(sem, count, like), kind="ext")
+
+    dma("ldxA", "s", lambda: T.xb[:, 0:512], lambda: T.x[:, 0:512], 128, [], [V("xb", 0, 512)])
+    dma("ldst", "s", lambda: T.sti[:], lambda: T.st[:], 8, [], [V("sti", 0, 2)], ["ldxA"])
+    dma("ldu", "s", lambda: T.ub[:], lambda: T.u[:], 128, [], [V("ub", 0, 512)], ["ldst"])
+    dma("ldxB", "s", lambda: T.xb[:, 512:1024], lambda: T.x[:, 512:1024], 128, [], [V("xb", 512, 1024)], ["ldu"])
+    dma("ldwc", "s", lambda: T.woq[:].bitcast(dt.uint8), lambda: T.wc[:], 256, [], [V("woq", 0, 512)], ["ldxB"])
+    dma("ldws", "s", lambda: T.wos[:], lambda: T.ws[:], 64, [], [V("wos", 0, 512)], ["ldwc"])
+    dma("ldv", "s", lambda: T.vb[:], lambda: T.v[:], 128, [], [V("vb", 0, 512)], ["ldws"])
+    quant("qxA", "xq0", "xs0", 0, 128, V("xb", 0, 512))
+    quant("qxB", "xq0", "xs0", 128, 256, V("xb", 512, 1024))
+    ship("sx0", peers["prev"], "xarr0", "xq0", "xs0", C, "xq0", "xs0", 0, B)
+    ship("sw0", peers["prev"], "warr0", "wq0", "wp0", 0, "woq", "wos", 0, 512)
+    ship("swd", peers["direct"], "warr1", "wq1", "wp1", 0, "woq", "wos", 0, 512)
+    arrive("ax0", "xarr0", peers["from_next"], [V("xq0", C, L), V("xs0", C, L)], "sx0s")
+    arrive("aw0", "warr0", peers["from_next"], [V("wq0", 0, 512), V("wp0", 0, 512)], "sw0s")
+
+    iota("ip0", V("pti", 0, 32), [[0, 2], [1, 16]], 0, 0)
+    iota("ip1", V("pti", 32, 64), [[1, 2], [0, 16]], 0, 0)
+    iota("ip2", V("pti", 64, 96), [[16, 2], [0, 2], [1, 8]], 0, 0)
+    iota("ip3", V("pti", 96, 112), [[0, 2], [2, 4], [16, 2]], 0, 0)
+    iota("ip4", V("pti", 112, 128), [[0, 2], [2, 4], [16, 2]], 1, 0)
+    iota("ip5", V("pti", 128, 160), [[16, 2], [1, 4], [0, 4]], 0, 0)
+    iota("ip6", V("pti", 160, 192), [[-L, 2], [1, 4], [L, 4]], 0, 0)
+    iota("iup", V("upf", 0, 16), [[16, 2], [32, 4], [0, 2]], 0, 0)
+    iota("i4", V("i4", 0, 8), [[-1, 2], [8, 2], [0, 2]], 0, 0)
+    iota("i16", V("i16", 0, 16), [[2, 8], [16, 2]], 0, 0)
+    iota("iq4", V("q4", 0, 64), [[0, 16], [4, 4]], 0, 0)
+    iota("ilb", V("lf", 28, 36), [[16, 8]], 15, 0)
+    iota("ie4", V("e4", 0, 128), [[0, 4], [4, 4], [0, 8]], 0, 0)
+    iota("ici", V("ci", 0, 128), [[0, 8], [1, 16]], -16, 0)
+    iota("iei", V("ei", 0, 128), [[1, 128]], 0, -1)
+    [o for o in ops if o["name"] == "sw0c"][0]["after"] += [o["name"] for o in ops if "g" in o["alts"] and o["kind"] == "c"]
+    transpose("pt", V("pt", 0, 192), V("pti", 0, 192))
+    PI, PK = V("pt", 0, 1), V("pt", 32, 33)
+    lin("lt", V("lf", 0, 4), V("i4", 4, 8), 1.0, V("pt", 64, 65))
+    lin("lc", V("lf", 4, 8), V("i4", 0, 4), 1.0, V("pt", 96, 97))
+    lin("lp", V("lf", 8, 24), V("i16", 0, 16), 1.0, PK)
+    lin("lk", V("lf", 24, 28), V("q4", 0, 4), 1.0, V("pt", 128, 129))
+    lin("q4t", V("q4t", 0, 64), V("q4", 0, 64), 1.0, V("pt", 160, 161))
+    copy("lu", V("lu", 0, 36), V("lf", 0, 36))
+    copy("upu", V("upu", 0, 16), V("upf", 0, 16))
+    memset("m_et", V("et", 0, 2048), 0.0, True)
+    lin("ea", V("ea", 0, 128), V("ei", 0, 128), 1.0, 0.0, "a", ACT.Abs)
+    for b in range(4):
+        lin("et%d" % b, V("et", 512 * b + b, 512 * b + 512, 4), V("ea", 0, 128), -1.0, 1.0, "a", ACT.Relu)
+    quant("qe0", "eq", "es", 0, 256, V("et", 0, 1024))
+    quant("qe1", "eq", "es", 256, 512, V("et", 1024, 2048))
+    memset("m_db", V("db", 0, 1), 0.0)
+    memset("m_a0", V("a0", 0, 1024, 4), -HUGE, True)
+    memset("m_a2", V("a0", 2, 1024, 4), 0.0, True)
+    memset("m_a3", V("a0", 3, 1024, 4), 0.0, True)
+    lin("rt", V("rt", 0, 128), V("ci", 0, 128), -HUGE, -15 * HUGE, "a", ACT.Relu)
+    memset("m_d1", V("d1", 0, 128), -1.0, True)
+    for t in range(R):
+        memset("m_ms%d" % t, V("ms%d" % t, 0, 4), 0.0)
+        memset("m_sx%d" % t, V("sx%d" % t, 0, 16), 0)
+
+    quant("qu", "uq", "us", 0, 128, V("ub", 0, 512))
+    UP = V("upu", 0, 16)
+    vec("pkq", lambda: g.vector.tensor_copy(T.u2q[:, 0:256].bitcast(dt.uint32),
+                                            T.uq[:, 0:128].bitcast(dt.uint32).indirect(ap(UP))),
+        ("gv", 256), [V("uq", 0, 128), UP], [V("u2q", 0, 256)])
+    gather("pks", V("u2s", 0, 256), V("us", 0, 128), UP, "va")
+    quant("qv", "vq", "vs", 0, 128, V("vb", 0, 512))
+
+    copy("stf", V("stf", 0, 2), V("sti", 0, 2))
+    for t in range(R):
+        lin("bi%d" % t, V("bi", 32 * t, 32 * t + 32), V("pt", 32, 64), float(L), V("stf", t, t + 1))
+    transpose("b2", V("b2", 0, 64), V("bi", 0, 64))
+    lin("b2i", V("b2i", 0, 64), V("b2", 0, 64), 1.0, PI)
+    tt("db", V("db", 1, 64), V("b2i", 0, 63), V("b2", 1, 64), ALU.subtract)
+
+    def scores(tag, t, bank, a, b, keep):
+        for h in range(2):
+            mm("ms%s%d%d" % (tag, t, h), bank + h, "u2q", "u2s", 128 * h, "xq%d" % t, "xs%d" % t, a, b)
+            scale("cs%s%d%d" % (tag, t, h), V("w2%d" % t, L * h + keep, L * h + b),
+                  V("ps", 512 * (bank + h) + keep - a, 512 * (bank + h) + b - a), 1.0)
+
+    scores("e", 0, 0, 0, C, 0)
+    for t in range(R):
+        n = lambda s: "%s%d" % (s, t)
+        BW = V("b2i", 32 * t, 32 * t + 32)
+        gtt(n("otf"), V(n("otf"), 0, 128), BW, V("lu", 0, 8), V("e4", 0, 128), ALU.add)
+        copy(n("otc"), V(n("otc"), 0, 128), V(n("otf"), 0, 128))
+        gtt(n("kk"), V(n("kk"), 0, 64), V("b2", 32 * t, 32 * t + 32), V("lu", 24, 28), V("q4t", 0, 64), ALU.add)
+        copy(n("of0"), V(n("of0"), 0, 4), V(n("kk"), 0, 4))
+        for S in range(2):
+            gtt(n("pen%d" % S), V(n("pen"), 128 * S, 128 * S + 128), V("db", 32 * t, 32 * t + 32),
+                V("lu", 8 + 8 * S, 16 + 8 * S), V("ci", 0, 128), ALU.is_equal)
+            scale(n("pes%d" % S), V("a0", 512 * S + 1, 512 * S + 512, 4), V(n("pen"), 128 * S, 128 * S + 128), PEN)
+        if t == 0:
+            scores("l", 0, 2, L - 128, L, C)
+        else:
+            arrive("ax1", "xarr1", peers["from_next"], [V("xq1", C, L), V("xs1", C, L)], "sx1s")
+            scores("l", 1, 2, 128, L, 128)
+        for b in range(4):
+            mm(n("mdv%d" % b), 4 + b, "eq", "es", 128 * b, n("xq"), n("xs"), 0, L)
+            scale(n("cdv%d" % b), V(n("dv"), L * b, L * b + L), V("ps", 512 * (4 + b), 512 * (4 + b) + L), 0.5, "a")
+        DV = V(n("dv"), 0, 4 * L)
+        gather(n("n0"), V(n("nn"), 0, 64), DV, V(n("of0"), 0, 4), "a")
+        for S in range(2):
+            m = lambda s: "%s%s%d" % (s, "AB"[S], t)
+            for j in range(2):
+                a = 512 * S + 256 * j
+                gather(m("tg%d" % j), V(n("tg"), a, a + 256), V(n("w2"), 16, 2 * L), V(n("otc"), a // 16, a // 16 + 16), "va")
+                transpose(m("tb%d" % j), V(n("tb"), a, a + 256), V(n("tg"), a, a + 256))
+                gtt(m("dd%d" % j), V(n("dd"), a, a + 256), V(n("w2"), 0, 2 * L), V(n("otc"), 64 + a // 16, 80 + a // 16),
+                    V(n("tb"), a, a + 256), ALU.subtract)
+                for e in (2 * j, 2 * j + 1):
+                    o, i = V(n("ab"), 512 * S + e, 512 * S + 512, 4), V(n("dd"), 512 * S + 128 * e, 512 * S + 128 * e + 128)
+                    op(m("ab%d" % e), {"a": (lambda o=o, i=i: g.scalar.activation(ap(o), ap(i), ACT.Abs), ("n", 128))}, [i], [o])
+            a, c = 512 * S, 128 * S
+            scan(m("ms"), V(n("ms"), a + 4, a + 516), V("a0", a, a + 512), V(n("ab"), a, a + 512), ALU.add, ALU.max)
+            scan(m("mb"), V(n("mb"), c, c + 128), V(n("ms"), a + 3, a + 512, 4), V("rt", 0, 128), ALU.min, ALU.max)
+            tt(m("nf"), V(n("nf"), c, c + 128), V(n("ms"), a + 7, a + 516, 4), V(n("mb"), c, c + 128), ALU.is_ge)
+            scan(m("cn"), V(n("cn"), c, c + 128), V(n("nf"), c, c + 128), V("d1", 0, 128), ALU.mult, ALU.add, 0.5)
+            lin(m("fb"), V(n("fb"), c, c + 128), V(n("cn"), c, c + 128), 1.0, 16.0, "va", None, V("lu", 28, 36))
+            transpose(m("ft"), V(n("ft"), c, c + 128), V(n("fb"), c, c + 128))
+            for k in range(max(8 * S, 1), 8 * S + 8):
+                gather(n("st%d_" % k), V(n("sx"), 16 * k, 16 * k + 16), V(n("ft"), 16 * k, 16 * k + 16),
+                       V(n("sx"), 16 * k - 16, 16 * k - 15))
+            h = 32 * S
+            for lo, hi in STAGES[t]:
+                if lo // 8 == S:
+                    r = lambda s: "%s%d_%d" % (s, lo, t)
+                    copy(r("cf"), V(n("cf"), 4 * lo, 4 * hi), V(n("sx"), 16 * lo, 16 * hi, 4))
+                    tt(r("po"), V(n("po"), 4 * lo, 4 * hi), V(n("cf"), 4 * lo, 4 * hi), V(n("kk"), 4 * lo, 4 * hi), ALU.add)
+                    copy(r("off"), V(n("off"), 4 * lo, 4 * hi), V(n("po"), 4 * lo, 4 * hi))
+            for j in range(2):
+                f, w = h + 16 * j, min(16, 60 - h - 16 * j)
+                gather(m("nn%d" % j), V(n("nn"), 16 * f + 64, 16 * (f + w) + 64), V(n("dv"), 16, 4 * L), V(n("off"), f, f + w), "a")
+                gtt(m("zt%d" % j), V(n("zt"), 16 * f, 16 * f + 256), DV, V(n("off"), f, f + 16),
+                    V(n("nn"), 16 * f, 16 * f + 256), ALU.add)
+            quant(m("qz"), n("zq"), n("zs"), c, c + 128, V(n("zt"), a, a + 512))
+        scale(n("pos"), V("pos", 16 * t, 16 * t + 16), V(n("po"), 0, 64, 4), 1.0)
+        if t == 1:
+            arrive("aw1", "warr1", peers["from_w1"], [V("wq1", 0, 512), V("wp1", 0, 512)], "sx1s")
+        nq, ns = "xq%d" % (t + 1), "xs%d" % (t + 1)
+        for S in range(2):
+            m = lambda s: "%s%s%d" % (s, "AB"[S], t)
+            a, c = 512 * S, 128 * S
+            for b in range(4):
+                k = 4 * S + b
+                mm(m("mr%d" % b), k, n("wq"), n("wp"), 128 * b, n("zq"), n("zs"), c, c + 128)
+                scale(m("ch%d" % b), V(n("ht"), a + b, a + 512, 4), V("ps", 512 * k, 512 * k + 128), 0.03125)
+            quant(m("qh"), n("hq"), n("hs"), c, c + 128, V(n("ht"), a, a + 512))
+            for b in range(4):
+                k = 4 * S + b
+                mm(m("mz%d" % b), k, "eq", "es", 128 * b, n("zq"), n("zs"), c, c + 128, True, False)
+                mm(m("mh%d" % b), k, "eq", "es", 128 * b, n("hq"), n("hs"), c, c + 128, False, True, m("mz%d" % b))
+                scale(m("cx%d" % b), V(n("xt"), a + b, a + 512, 4), V("ps", 512 * k, 512 * k + 128), 1.0)
+            quant(m("qx"), nq, ns, c, c + 128, V(n("xt"), a, a + 512))
+            if S == 0 and t == 0:
+                scores("e", 1, 0, 0, 128, 0)
+            if S == 0 and t == 1:
+                mm("myA", 0, "vq", "vs", 0, nq, ns, 0, 128)
+                scale("cyA", V("yb", 0, 128), V("ps", 0, 128), 1.0)
+            if S == 0 and t == 0:
+                ship("sx1", peers["prev"], "xarr1", "xq1", "xs1", C, "xq1", "xs1", 0, B)
+                ship("swf", peers["prev"] if peers["forward"] else None, "warr1", "wq1", "wp1", 0, "wq0", "wp0", 0, 512)
+    mm("myB", 1, "vq", "vs", 0, "xq2", "xs2", 128, 256)
+    scale("cyB", V("yb", 128, 256), V("ps", 512, 640), 1.0)
+
+    dma("ool", "s", lambda: T.ol[:], lambda: T.pos[0:128:16, :], 1, [V("pos", 0, 32)], [])
+    for S in range(2):
+        c = 128 * S
+        dma("ooc%d" % S, "sa", lambda c=c: T.oc[:, 4 * c:4 * c + 512], lambda c=c: T.xq2[:, c:c + 128].bitcast(dt.uint8), 64,
+            [V("xq2", c, c + 128)], [])
+        dma("oy%d" % S, "sa", lambda c=c: T.y[:, c:c + 128], lambda c=c: T.yb[:, c:c + 128], 64, [V("yb", c, c + 128)], [])
+    for k in range(4):
+        dma("osc%d" % k, "sa", lambda k=k: T.osc[4 * k:4 * k + 4, :], lambda k=k: T.xs2[32 * k:32 * k + 4, :], 1,
+            [V("xs2", 0, C)], [])
+    return ops
+
+
+def depend(ops):
+    index = {o["name"]: i for i, o in enumerate(ops)}
+    seen = {}
+    for i, o in enumerate(ops):
+        dep = set()
+        acc = index[o["acc"]] if o["acc"] else None
+        for views, writes in ((o["rd"], False), (o["wr"], True)):
+            for v in views:
+                m = span(v)
+                for (m2, j, w2) in seen.get(v[0], []):
+                    if m & m2 and (writes or w2) and j != acc and j != i:
+                        dep.add(j)
+        for views, writes in ((o["rd"], False), (o["wr"], True)):
+            for v in views:
+                m = span(v)
+                old = seen.get(v[0], [])
+                if writes:
+                    old = [e for e in old if e[0] & ~m]
+                seen[v[0]] = old + [(m, i, writes)]
+        o["dep"] = dep
+        o["aft"] = set(index[a] for a in o["after"]) | (set() if acc is None else {acc})
+    return index
+
+
+def emit(g, T, ops, order):
+    queues = {"v": g.vector, "a": g.scalar, "p": g.tensor, "s": g.sync, "g": g}
+    known = {q: set() for q in queues}
+    closure, waits, before, needed = {}, {}, {}, set()
+    for i, o in enumerate(ops):
+        if o["kind"] == "ext":
+            closure[i] = {i}
+    for i, q in order:
+        need = [d for d in ops[i]["dep"] if d not in known[q]]
+        need = sorted(d for d in need if not any(e != d and d in closure[e] for e in need))
+        waits[i] = need
+        for d in need:
+            known[q] |= closure[d]
+            needed.add(d)
+        before[i] = set(known[q])
+        closure[i] = before[i] | {i}
+    stores = [i for i, q in order if ops[i]["kind"] == "dma" and not ops[i]["wr"]]
+    needed |= set(stores)
+    last, count, mark = [None] * NPOOL, [0] * NPOOL, {}
+    for i, o in enumerate(ops):
+        if o["kind"] == "ext":
+            mark[i] = o["ext"][:2]
+    sent = 0
+    for i, q in order:
+        for d in waits[i]:
+            queues[q].wait_ge(T.sem[mark[d][0]], mark[d][1])
+        ins = ops[i]["alts"][q][0]()
+        sent += ops[i].get("eng", 0)
+        if i in needed:
+            s = [k for k in range(NPOOL) if last[k] is None or last[k] in before[i]][0]
+            step = 16 if ops[i]["kind"] == "dma" else 1
+            last[s] = i
+            count[s] += step
+            mark[i] = ("s%d" % s, count[s])
+            ins.then_inc(T.sem["s%d" % s], step)
+    for i in stores:
+        g.sync.wait_ge(T.sem[mark[i][0]], mark[i][1])
+    g.wait_ge(T.sem["sent"], sent)
+
+
+def wiring(T, topo, rank):
+    cores, n = T.cores, len(T.cores)
+
+    def engines(a, b):
+        e = topo.engines(cores[a % n], cores[b % n])
+        return e[len(e) // 2:] if together(a, b) else e
+
+    def together(a, b):
+        return topo.chip(cores[a % n]) == topo.chip(cores[b % n])
+
+    def peer(b):
+        e = engines(rank, b)
+        rid, pid = topo.addr(cores[b % n])[:2]
+        return (rid, pid, sum(1 << k for k in e), len(e))
+
+    def relayed(q):
+        return together(q, q + 1) and not together(q, q + 2)
+
+    return {"prev": peer(rank - 1), "direct": None if relayed(rank - 2) else peer(rank - 2), "forward": relayed(rank - 1),
+            "from_next": 2 * len(engines(rank + 1, rank)),
+            "from_w1": 2 * len(engines(rank + (1 if relayed(rank) else 2), rank))}
+
+
+def rank_program(g, core, T, topo):
+    rank = T.rank_of(core)
+    if rank is None:
+        return
+    ops = program(g, T, wiring(T, topo, rank))
+    depend(ops)
+    order = [(int(w[:-1], 16), w[-1]) for w in ORDER.split()]
+    emit(g, T, ops, [e for e in order if ops[e[0]]["kind"] != "none"])

@@ -1,60 +1,56 @@
+import math
+
 from concourse.mybir import dt, AluOpType, ActivationFunctionType
 
 ALU = AluOpType
 ACT = ActivationFunctionType
 C, B, L, R = 256, 96, 352, 2
 Q4, U8, F32, BF, I32, U16 = "float8_e4m3fn_x4", "uint8", "float32", "bfloat16", "int32", "uint16"
+PAD = 16
+RUNS = ((1, 5), (6, 4), (10, 6))
+PLACES = (((1, 4), (4, 6), (6, 10), (10, 14), (14, 16)),) * 2
+TEMPLATES = (((0, 5), (5, 7), (7, 11), (11, 15), (15, 16)),) * 2
+SUMS = (((0, 4), (4, 6), (6, 10), (10, 14), (14, 16)), ((0, 4), (4, 8), (8, 12), (12, 14), (14, 16)))
+DIRECT = tuple(range(16))
+OWN = 336
+CUT = (96, 128)
+PAIRS = 16 * max(_r[1] for _r in RUNS)
 
 SCRATCH = {
     "ps": ("psum", [128, 4096], F32),
     "xb": ("sbuf", [128, 4 * C], BF), "ub": ("sbuf", [128, 512], BF), "vb": ("sbuf", [128, 512], BF),
-    "sti": ("sbuf", [128, 2], I32), "stf": ("sbuf", [128, 2], F32),
+    "sti": ("sbuf", [128, 2], I32), "stf": ("sbuf", [128, 4], F32),
     "uq": ("sbuf", [128, 128], Q4), "us": ("sbuf", [128, 128], U8),
     "u2q": ("sbuf", [128, 256], Q4), "u2s": ("sbuf", [128, 256], U8),
     "vq": ("sbuf", [128, 128], Q4), "vs": ("sbuf", [128, 128], U8),
     "woq": ("sbuf", [128, 512], Q4), "wos": ("sbuf", [128, 512], U8),
-    "ei": ("sbuf", [128, 128], BF), "ea": ("sbuf", [128, 128], BF), "et": ("sbuf", [128, 2048], BF),
-    "eq": ("sbuf", [128, 512], Q4), "es": ("sbuf", [128, 512], U8),
-    "pti": ("sbuf", [128, 192], F32), "pt": ("sbuf", [128, 192], F32),
-    "i4": ("sbuf", [128, 8], F32), "i16": ("sbuf", [128, 16], F32),
-    "q4": ("sbuf", [128, 64], F32), "q4t": ("sbuf", [128, 64], F32),
-    "lf": ("sbuf", [128, 36], F32), "lu": ("sbuf", [128, 36], U16),
+    "hq": ("sbuf", [128, 512 - OWN], Q4), "hs": ("sbuf", [128, 512 - OWN], U8),
+    "et": ("sbuf", [128, 516], BF), "eq": ("sbuf", [128, 512], Q4), "es": ("sbuf", [128, 512], U8),
+    "pi": ("sbuf", [128, 8], I32), "pf": ("sbuf", [128, 16], F32),
+    "xf": ("sbuf", [128, 144], F32), "idt": ("sbuf", [128, 144], F32), "ci": ("sbuf", [128, 240], F32),
+    "yy": ("sbuf", [128, 4], F32), "q4t": ("sbuf", [128, 128], F32),
+    "lf": ("sbuf", [128, 20], F32), "lu": ("sbuf", [128, 36], U16),
+    "xx": ("sbuf", [128, 248], F32), "ot": ("sbuf", [128, 128], U16),
+    "ms": ("sbuf", [128, 964], F32), "tt": ("sbuf", [128, 2 * PAIRS * len(RUNS)], F32),
     "upf": ("sbuf", [128, 16], I32), "upu": ("sbuf", [128, 16], U16),
-    "e4": ("sbuf", [128, 128], F32), "ci": ("sbuf", [128, 128], F32),
-    "bi": ("sbuf", [128, 64], F32), "b2": ("sbuf", [128, 64], F32),
-    "b2i": ("sbuf", [128, 64], F32), "db": ("sbuf", [128, 64], F32),
-    "a0": ("sbuf", [128, 1024], BF), "rt": ("sbuf", [128, 128], F32), "d1": ("sbuf", [128, 128], BF),
+    "bi": ("sbuf", [128, 64], F32), "b2": ("sbuf", [128, 64], F32), "b3": ("sbuf", [128, 64], F32),
+    "bo": ("sbuf", [128, 64], F32), "db": ("sbuf", [128, 32], F32),
+    "a0": ("sbuf", [128, 960], BF), "rt": ("sbuf", [128, 128], F32), "d1": ("sbuf", [128, 240], F32),
     "pos": ("sbuf", [128, 32], F32), "yb": ("sbuf", [128, C], F32),
-    "xq2": ("sbuf", [128, C], Q4), "xs2": ("sbuf", [128, C], U8),
+    "xq2": ("sbuf", [128, L], Q4), "xs2": ("sbuf", [128, L], U8),
 }
 for _t in range(R):
     for _n, _w, _d in (("xq", L, Q4), ("xs", L, U8), ("wq", 512, Q4), ("wp", 512, U8), ("w2", 2 * L, F32),
-                       ("otf", 128, F32), ("otc", 128, U16), ("kk", 64, F32), ("of0", 4, U16), ("pen", 256, BF),
-                       ("tg", 1024, F32), ("tb", 1024, F32), ("dd", 1024, F32), ("ab", 1024, F32),
-                       ("ms", 1028, F32), ("mb", 256, F32), ("nf", 256, BF), ("cn", 256, BF), ("fb", 256, F32),
-                       ("ft", 256, F32), ("sx", 256, U16), ("cf", 64, F32), ("po", 64, F32), ("off", 64, U16),
-                       ("dv", 4 * L, F32), ("nn", 1024, F32), ("zt", 1024, BF), ("zq", C, Q4), ("zs", C, U8),
+                       ("kk", 136, F32), ("cg", 136, F32), ("pen", 240, F32),
+                       ("tg", 960, F32), ("tb", 960, F32), ("dd", 960, F32), ("ab", 960, F32),
+                       ("mb", 240, F32), ("nf", 240, F32), ("cn", 240, F32), ("fu", 48, U16),
+                       ("sx", 256, U16), ("cf", 8, F32), ("po", 136, F32),
+                       ("off", 68, U16),
+                       ("dv", PAD + 4 * L, F32), ("nn", 1024, F32), ("zt", 1024, BF), ("zq", C, Q4), ("zs", C, U8),
                        ("ht", 1024, BF), ("hq", C, Q4), ("hs", C, U8), ("xt", 1024, BF)):
         SCRATCH["%s%d" % (_n, _t)] = ("sbuf", [128, _w], _d)
-NPOOL = 120
-SEMAPHORES = ["s%d" % _i for _i in range(NPOOL)] + ["sent", "xarr0", "xarr1", "warr0", "warr1"]
-
-STAGES = (((0, 4), (4, 8), (8, 12), (12, 16)),) * 2
-ORDER = """
-0s 1s 32v 2s 3s 18g 13g 4s 35v 1ag 15g 31v 12g 27v 28v 37v 14g 11g 17g 16g 30v 36v 1bg 7v 3ev 9g 3av 20v 3ca 33v 23v ag
-3fv 40a 3bv 24a 1fg 8v 41v 46p 19g 44p 1cg 21a 22v 29a 5s 6s 42a 25v 1dg 26v 43v 4av 2aa 1eg 48v 2da 2ca 49v 45a 4cv 2ba
-2fv 47a 34a 2ev bg cg 4bv 50p 52p 51a 54p 53a dg 4da 4ev 58p eg 62v 5da 56p 5ap 63v 7fa 5ev 84a 64v 65a 5fv 66a 85v 60a
-61a 80v 57a 67v 5ba 86v 68v 88a 81v 4fa 87a 69v 83a 82a 6av 89v 6ba 6cv 59a 55a 8av 5ca 6dv 6ev 8bv 6fv 8cv 70v 8da 74v
-71v 75v 72v 76v 73v 7aa 8ev 77v 8fv 78v 90v 79v 91v 7ca 7bv 7dv 92v 7ev 93v a3p 97v a5p 94v a4a a9p 98v a7p a6a 95v acp
-aav afp 99v a8a b5p abv 9da b2p 96v b0p 9av b3p adp b1v b6p 9bv b4a aev b7a 9cv a2a b8v 9fa 9ev bbp bca a0v a1v 3dv bdg
-beg c1p c2a bfg c3p ddv c7p c5p c4a cap c8v c6a c0g 39v cdp 38v dea d3p c9v d0p d7v d1p d2a cep dbv cbp d4p cfa d5v b9p
-cca dca d6v d9v e0p d8v e2p dav e1a eap e3v baa f2a edv e6p e4p 114a eev f3v 10fa efv f4v f0a 110v e8p f1a f5a f6a 115v
-f7v e9a e5a eba 116v f8v 118a 117a 111v f9v 113a 112a fav 119v fba e7a fcv 11av eca fdv 11bv fev 11cv ffv 100v 11da 104v
-101v 11ev 102v 105v 103v 106v 11fv 10aa 107v 120v 108v 121v 109v 122v 10ca 10bv 123v 127v 124v 128v 125v 129v 126v 12da
-10dv 12av 10ev 12bv 134p 12ev 138p 135a 136p 13ap 137a 12cv 139v 12fa 143p 13bv 132a 164s 13dp 13cv 146p 140p 141p 130v
-13ep 147p 13fa 131v 148a 144p 145v 142a 152p 14ep 153a 14cp 149v 165s 14fa 150p 15ep 151a 158p 14dv 154v 155p 15bp 15cp
-159p 15dv 15fp 156p 15aa 160a 157v 161v 16aa 169s 14ap 162p 14bv 167a 16ca 166s 163v 16ba 168s
-"""
+NPOOL = 140
+SEMAPHORES = ["s%d" % _i for _i in range(NPOOL)] + ["sent", "xarr0", "xarr1", "warr0", "warr1", "hop"]
 HUGE, PEN = 2.0 ** 92, 2.0 ** 88
 
 
@@ -96,14 +92,26 @@ def program(g, T, peers):
     def aps(*xs):
         return [x for x in xs if isinstance(x, tuple)]
 
-    def memset(name, o, val, half=False):
-        vec(name, lambda: g.vector.memset(ap(o), val), ("n", width(o) * (0.5 if half else 1)), [], [o])
+    def memset(name, o, val):
+        f = 0.5 if SCRATCH[o[0]][2] in (BF, U16) else 1
+        alts = {"v": (lambda: g.vector.memset(ap(o), val), ("n", width(o) * f))}
+        row = V("xf" if width(o) <= 144 else "ci", 0, width(o))
+        if width(o) <= 240:
+            alts["a"] = (lambda: g.scalar.activation(ap(o), ap(row), ACT.Identity, bias=val, scale=0.0), ("n", width(o)))
+        op(name, alts, [row] if "a" in alts else [], [o])
 
     def copy(name, o, i):
         vec(name, lambda: g.vector.tensor_copy(ap(o), ap(i)), ("n", width(o)), [i], [o])
 
     def tt(name, o, a, b, alu):
         vec(name, lambda: g.vector.tensor_tensor(ap(o), ap(a), ap(b), alu), ("n", 2 * width(o)), [a, b], [o])
+
+    def ts(name, o, i, s1, op0, s2=None, op1=None):
+        if op1 is None:
+            fn = lambda: g.vector.tensor_scalar(ap(o), ap(i), sc(s1), None, op0)
+        else:
+            fn = lambda: g.vector.tensor_scalar(ap(o), ap(i), sc(s1), sc(s2), op0, op1)
+        vec(name, fn, ("n", width(o)), [i] + aps(s1, s2), [o])
 
     def gtt(name, o, win, off, b, alu):
         vec(name, lambda: g.vector.tensor_tensor(ap(o), ap(win).indirect(ap(off)), ap(b), alu), ("gv", width(o)),
@@ -129,19 +137,16 @@ def program(g, T, peers):
         psum = [i] if i[0] == "ps" else []
         op(name, alts, [] if psum else [i], [o] + psum)
 
-    def lin(name, o, i, k, bias, queues="va", func=None, off=None):
-        src = (lambda: ap(i)) if off is None else (lambda: ap(i).indirect(ap(off)))
+    def lin(name, o, i, k, bias, queues="va"):
         alts = {}
         if "v" in queues:
-            alts["v"] = (lambda: g.vector.tensor_scalar(ap(o), src(), k, sc(bias), ALU.mult, ALU.add),
-                         ("n" if off is None else "gv", width(o)))
+            alts["v"] = (lambda: g.vector.tensor_scalar(ap(o), ap(i), k, sc(bias), ALU.mult, ALU.add), ("n", width(o)))
         if "a" in queues:
-            alts["a"] = (lambda: g.scalar.activation(ap(o), src(), func or ACT.Identity, bias=sc(bias), scale=k),
-                         ("n" if off is None else "ga", width(o)))
-        op(name, alts, [i] + aps(bias, off), [o])
+            alts["a"] = (lambda: g.scalar.activation(ap(o), ap(i), ACT.Identity, bias=sc(bias), scale=k), ("n", width(o)))
+        op(name, alts, [i] + aps(bias), [o])
 
-    def scan(name, o, d0, d1, op0, op1, f=1.0):
-        vec(name, lambda: g.vector.tensor_tensor_scan(ap(o), ap(d0), ap(d1), 0.0, op0, op1), ("n", width(o) * f),
+    def scan(name, o, d0, d1, op0, op1):
+        vec(name, lambda: g.vector.tensor_tensor_scan(ap(o), ap(d0), ap(d1), 0.0, op0, op1), ("n", width(o)),
             [d0, d1], [o])
 
     def transpose(name, o, i):
@@ -157,12 +162,12 @@ def program(g, T, peers):
         op(name, {"p": (lambda: g.tensor.matmul_mx(ap(o), ap(a), ap(b), ap(c), ap(d), start, stop), ("mm", rb - ra))},
            [a, b, c, d], [o], acc=acc)
 
-    def iota(name, o, pattern, base, cm):
+    def iota(name, o, pattern, base, cm, after=()):
         if SCRATCH[o[0]][2] == I32:
             fn = lambda: g.iota(ap(o), pattern, base, cm)
         else:
             fn = lambda: g.iota(ap(o), pattern, base, cm, allow_small_or_imprecise_dtypes=True)
-        op(name, {"g": (fn, ("io", width(o)))}, [], [o])
+        op(name, {"g": (fn, ("io", width(o)))}, [], [o], after=after)
 
     def dma(name, queues, dst, src, kb, rd, wr, after=()):
         alts = {}
@@ -177,74 +182,90 @@ def program(g, T, peers):
 
     last_remote = []
 
-    def ship(name, peer, sem, dq, ds, da, sq, ss, sa, n):
+    def ship(name, peer, sem, dq, ds, da, sq, ss, sa, n, scales_first=False):
         a, b, c, d = V(dq, da, da + n), V(sq, sa, sa + n), V(ds, da, da + n), V(ss, sa, sa + n)
-        kind = "none" if peer is None else "rem"
-        op(name + "c", {"g": (lambda: g.remote_dma(codes(a), codes(b), T.sem[sem], T.sem["sent"], peer[1], peer[0], peer[2]),
-                              ("rem", n / 2.0))}, [b], [], after=last_remote[-1:], kind=kind)
-        op(name + "s", {"g": (lambda: g.remote_dma(ap(c), ap(d), T.sem[sem], T.sem["sent"], peer[1], peer[0], peer[2]),
-                              ("rem", n / 8.0))}, [d], [], after=[name + "c"], kind=kind)
-        ops[-1]["eng"] = ops[-2]["eng"] = 0 if peer is None else peer[3]
-        last_remote.append(name + "s")
+        sems = sem if scales_first else (sem, sem)
+        calls = [("c", b, lambda: g.remote_dma(codes(a), codes(b), T.sem[sems[1]], T.sem["sent"], peer[1], peer[0], peer[2])),
+                 ("s", d, lambda: g.remote_dma(ap(c), ap(d), T.sem[sems[0]], T.sem["sent"], peer[1], peer[0], peer[2]))]
+        for tag, src, fn in (calls[::-1] if scales_first else calls):
+            op(name + tag, {"g": (fn, ("rem", 0))}, [src], [], after=last_remote[-1:], kind="none" if peer is None else "rem")
+            ops[-1]["eng"] = 0 if peer is None else peer[3]
+            last_remote.append(name + tag)
 
-    def arrive(name, sem, count, wr, like):
-        op(name, {"x": (None, ("arr", like))}, [], wr, ext=(sem, count, like), kind="ext")
+    def arrive(name, sem, count, wr, like, more=0.0):
+        op(name, {"x": (None, ("arr", more))}, [], wr, after=[like], ext=(sem, count), kind="ext")
 
     dma("ldxA", "s", lambda: T.xb[:, 0:512], lambda: T.x[:, 0:512], 128, [], [V("xb", 0, 512)])
-    dma("ldst", "s", lambda: T.sti[:], lambda: T.st[:], 8, [], [V("sti", 0, 2)], ["ldxA"])
-    dma("ldu", "s", lambda: T.ub[:], lambda: T.u[:], 128, [], [V("ub", 0, 512)], ["ldst"])
-    dma("ldxB", "s", lambda: T.xb[:, 512:1024], lambda: T.x[:, 512:1024], 128, [], [V("xb", 512, 1024)], ["ldu"])
-    dma("ldwc", "s", lambda: T.woq[:].bitcast(dt.uint8), lambda: T.wc[:], 256, [], [V("woq", 0, 512)], ["ldxB"])
-    dma("ldws", "s", lambda: T.wos[:], lambda: T.ws[:], 64, [], [V("wos", 0, 512)], ["ldwc"])
-    dma("ldv", "s", lambda: T.vb[:], lambda: T.v[:], 128, [], [V("vb", 0, 512)], ["ldws"])
-    quant("qxA", "xq0", "xs0", 0, 128, V("xb", 0, 512))
-    quant("qxB", "xq0", "xs0", 128, 256, V("xb", 512, 1024))
-    ship("sx0", peers["prev"], "xarr0", "xq0", "xs0", C, "xq0", "xs0", 0, B)
-    ship("sw0", peers["prev"], "warr0", "wq0", "wp0", 0, "woq", "wos", 0, 512)
-    ship("swd", peers["direct"], "warr1", "wq1", "wp1", 0, "woq", "wos", 0, 512)
-    arrive("ax0", "xarr0", peers["from_next"], [V("xq0", C, L), V("xs0", C, L)], "sx0s")
-    arrive("aw0", "warr0", peers["from_next"], [V("wq0", 0, 512), V("wp0", 0, 512)], "sw0s")
+    dma("ldst", "a", lambda: T.sti[:], lambda: T.st[:], 8, [], [V("sti", 0, 2)])
+    dma("ldu", "a", lambda: T.ub[:], lambda: T.u[:], 256, [], [V("ub", 0, 512)], ["ldst"])
+    dma("ldwd", "s", lambda: T.woq[:, OWN:512].bitcast(dt.uint8), lambda: T.wc[:, 4 * OWN:2048], 340, [],
+        [V("woq", OWN, 512)], ["ldxA"])
+    dma("ldws", "s", lambda: T.wos[:], lambda: T.ws[:], 410, [], [V("wos", 0, 512)], ["ldwd"])
+    dma("ldxB", "a", lambda: T.xb[:, 512:1024], lambda: T.x[:, 512:1024], 540, [], [V("xb", 512, 1024)], ["ldu"])
+    dma("ldwc", "s", lambda: T.woq[:, 0:OWN].bitcast(dt.uint8), lambda: T.wc[:, 0:4 * OWN], 700, [], [V("woq", 0, OWN)], ["ldws"])
 
-    iota("ip0", V("pti", 0, 32), [[0, 2], [1, 16]], 0, 0)
-    iota("ip1", V("pti", 32, 64), [[1, 2], [0, 16]], 0, 0)
-    iota("ip2", V("pti", 64, 96), [[16, 2], [0, 2], [1, 8]], 0, 0)
-    iota("ip3", V("pti", 96, 112), [[0, 2], [2, 4], [16, 2]], 0, 0)
-    iota("ip4", V("pti", 112, 128), [[0, 2], [2, 4], [16, 2]], 1, 0)
-    iota("ip5", V("pti", 128, 160), [[16, 2], [1, 4], [0, 4]], 0, 0)
-    iota("ip6", V("pti", 160, 192), [[-L, 2], [1, 4], [L, 4]], 0, 0)
-    iota("iup", V("upf", 0, 16), [[16, 2], [32, 4], [0, 2]], 0, 0)
-    iota("i4", V("i4", 0, 8), [[-1, 2], [8, 2], [0, 2]], 0, 0)
-    iota("i16", V("i16", 0, 16), [[2, 8], [16, 2]], 0, 0)
-    iota("iq4", V("q4", 0, 64), [[0, 16], [4, 4]], 0, 0)
-    iota("ilb", V("lf", 28, 36), [[16, 8]], 15, 0)
-    iota("ie4", V("e4", 0, 128), [[0, 4], [4, 4], [0, 8]], 0, 0)
-    iota("ici", V("ci", 0, 128), [[0, 8], [1, 16]], -16, 0)
-    iota("iei", V("ei", 0, 128), [[1, 128]], 0, -1)
-    [o for o in ops if o["name"] == "sw0c"][0]["after"] += [o["name"] for o in ops if "g" in o["alts"] and o["kind"] == "c"]
-    transpose("pt", V("pt", 0, 192), V("pti", 0, 192))
-    PI, PK = V("pt", 0, 1), V("pt", 32, 33)
-    lin("lt", V("lf", 0, 4), V("i4", 4, 8), 1.0, V("pt", 64, 65))
-    lin("lc", V("lf", 4, 8), V("i4", 0, 4), 1.0, V("pt", 96, 97))
-    lin("lp", V("lf", 8, 24), V("i16", 0, 16), 1.0, PK)
-    lin("lk", V("lf", 24, 28), V("q4", 0, 4), 1.0, V("pt", 128, 129))
-    lin("q4t", V("q4t", 0, 64), V("q4", 0, 64), 1.0, V("pt", 160, 161))
-    copy("lu", V("lu", 0, 36), V("lf", 0, 36))
+    iota("ipi", V("pi", 0, 1), [[0, 1]], 0, 1)
+    iota("ixf", V("xf", 0, 144), [[1, 144]], 0, 0, ["ipi"])
+    iota("iup", V("upf", 0, 16), [[16, 2], [32, 4], [0, 2]], 0, 0, ["ixf"])
+    iota("iyy", V("yy", 0, 4), [[2, 2], [64, 2]], 0, 0, ["iup"])
+    quant("qxA", "xq0", "xs0", 0, 128, V("xb", 0, 512))
+    quant("qxB", "xq0", "xs0", 128, C, V("xb", 512, 1024))
+    iota("ici", V("ci", 0, 240), [[0, 15], [1, 16]], -16, 0, ["iyy"])
+    last_remote.append("ici")
+    ship("sx0", peers["prev"], "xarr0", "xq0", "xs0", C, "xq0", "xs0", 0, B)
+    ship("swh", peers["helper"], "hop", "hq", "hs", 0, "woq", "wos", OWN, 512 - OWN)
+    ship("sw0", peers["prev"], "warr0", "wq0", "wp0", 0, "woq", "wos", 0, 512 if peers["helper"] is None else OWN)
+    arrive("ax0", "xarr0", peers["from_next"], [V("xq0", C, L), V("xs0", C, L)], "sx0s")
+    arrive("aw0", "warr0", peers["from_w0"], [V("wq0", 0, 512), V("wp0", 0, 512)], "sw0s", PLAN["layer"])
+    arrive("ah", "hop", peers["from_prev"], [V("hq", 0, 512 - OWN), V("hs", 0, 512 - OWN)], "swhs")
+    for k0, nk in RUNS + ((16, 1),):
+        iota("iq%d" % k0, V("q4t", 8 * k0 - 8, 8 * (k0 + nk) - 8), [[-16, nk], [4, 4], [0, 2]], PAD, 0, ["sw0s"])
+        last_remote.append("iq%d" % k0)
+    ship("swo", peers["direct"], "warr0", "wq0", "wp0", OWN, "hq", "hs", 0, 512 - OWN)
+    ship("swd", peers["direct"], "warr1", "wq1", "wp1", 0, "woq", "wos", 0, 512)
+
+    for j, (shift, mask) in enumerate(((0, 15), (4, 1), (3, 1), (0, 3), (2, 3), (0, 1))):
+        ts("pi%d" % j, V("pi", 1 + j, 2 + j), V("pi", 0, 1), shift, ALU.logical_shift_right, mask, ALU.bitwise_and)
+    copy("pf", V("pf", 0, 7), V("pi", 0, 7))
+    P, PI, GP, HI, P4, PQ, ODD, GL, H128, LB, LA, SK = [V("pf", j, j + 1) for j in range(12)]
+    lin("gl", GL, GP, float(L), 0.0)
+    lin("h128", H128, HI, float(PAIRS), 0.0)
+    lin("lb", LB, PI, 4.0, GP)
+    ts("la1", V("pf", 13, 14), GP, ODD, ALU.subtract, 3.0, ALU.mult)
+    lin("la", LA, V("pf", 13, 14), 1.0, LB)
+    lin("sk1", V("pf", 12, 13), P4, float(L), PQ)
+    ts("sk", SK, V("pf", 12, 13), PI, ALU.subtract, GL, ALU.subtract)
+    lin("lfa", V("lf", 0, 4), V("yy", 0, 4), 1.0, LA)
+    lin("lfb", V("lf", 4, 8), V("yy", 0, 4), 1.0, LB)
+    lin("lfo", V("lf", 8, 10), V("xf", 0, 2), 2.0, LB)
+    lin("lfh", V("lf", 10, 12), V("xf", 0, 2), 0.0, H128)
+    lin("lfq", V("lf", 12, 20), V("xf", 0, 8), 2.0, HI)
+    copy("lu", V("lu", 0, 20), V("lf", 0, 20))
+    copy("luk", V("lu", 20, 36), V("xf", 0, 16))
     copy("upu", V("upu", 0, 16), V("upf", 0, 16))
-    memset("m_et", V("et", 0, 2048), 0.0, True)
-    lin("ea", V("ea", 0, 128), V("ei", 0, 128), 1.0, 0.0, "a", ACT.Abs)
+    lin("idt", V("idt", 0, 144), V("xf", 0, 144), 1.0, H128)
+    memset("m_et", V("et", 0, 516), 0.0)
+    ts("et", V("et", 3, 515, 4), V("xf", 0, 128), P, ALU.is_equal)
     for b in range(4):
-        lin("et%d" % b, V("et", 512 * b + b, 512 * b + 512, 4), V("ea", 0, 128), -1.0, 1.0, "a", ACT.Relu)
-    quant("qe0", "eq", "es", 0, 256, V("et", 0, 1024))
-    quant("qe1", "eq", "es", 256, 512, V("et", 1024, 2048))
-    memset("m_db", V("db", 0, 1), 0.0)
-    memset("m_a0", V("a0", 0, 1024, 4), -HUGE, True)
-    memset("m_a2", V("a0", 2, 1024, 4), 0.0, True)
-    memset("m_a3", V("a0", 3, 1024, 4), 0.0, True)
-    lin("rt", V("rt", 0, 128), V("ci", 0, 128), -HUGE, -15 * HUGE, "a", ACT.Relu)
-    memset("m_d1", V("d1", 0, 128), -1.0, True)
+        quant("qe%d" % b, "eq", "es", 128 * b, 128 * b + 128, V("et", 3 - b, 515 - b))
+    for e, val in ((0, -HUGE), (2, 0.0), (3, 0.0)):
+        memset("m_a%d" % e, V("a0", e, 960, 4), val)
+    memset("m_rt", V("rt", 0, 128), 0.0)
+    memset("m_rt0", V("rt", 0, 128, 16), HUGE)
+    memset("m_d1", V("d1", 0, 240), -1.0)
+    memset("m_d15", V("d1", 15, 240, 16), 15.0)
+    for S, (k0, nk) in enumerate(RUNS):
+        lin("d1_%d" % k0, V("d1", 16 * k0 - 1, 16 * (k0 + nk - 2), 16), V("xf", 16, 16 * nk, 16), 1.0, 15.0)
+        tb = 2 * PAIRS * S
+        if 16 * nk < PAIRS:
+            memset("m_ta%d" % S, V("tt", tb + 16 * nk, tb + PAIRS), 0.0)
+        if nk % 2:
+            memset("m_tb%d" % S, V("tt", tb + PAIRS + 16 * (nk - 2), tb + PAIRS + 16 * nk), 0.0)
+    memset("m_db", V("db", 31, 32), 0.0)
+    memset("m_xx", V("xx", 240, 248), 0.0)
+    memset("m_ms", V("ms", 0, 4), 0.0)
     for t in range(R):
-        memset("m_ms%d" % t, V("ms%d" % t, 0, 4), 0.0)
-        memset("m_sx%d" % t, V("sx%d" % t, 0, 16), 0)
+        memset("m_dv%d" % t, V("dv%d" % t, 0, PAD), 0.0)
 
     quant("qu", "uq", "us", 0, 128, V("ub", 0, 512))
     UP = V("upu", 0, 16)
@@ -252,114 +273,142 @@ def program(g, T, peers):
                                             T.uq[:, 0:128].bitcast(dt.uint32).indirect(ap(UP))),
         ("gv", 256), [V("uq", 0, 128), UP], [V("u2q", 0, 256)])
     gather("pks", V("u2s", 0, 256), V("us", 0, 128), UP, "va")
-    quant("qv", "vq", "vs", 0, 128, V("vb", 0, 512))
 
     copy("stf", V("stf", 0, 2), V("sti", 0, 2))
+    lin("stg", V("stf", 2, 4), V("stf", 0, 2), 1.0, GL)
     for t in range(R):
-        lin("bi%d" % t, V("bi", 32 * t, 32 * t + 32), V("pt", 32, 64), float(L), V("stf", t, t + 1))
+        lin("bi%d" % t, V("bi", 32 * t, 32 * t + 32), V("xf", 0, 32), 0.0, V("stf", 2 + t, 3 + t))
     transpose("b2", V("b2", 0, 64), V("bi", 0, 64))
-    lin("b2i", V("b2i", 0, 64), V("b2", 0, 64), 1.0, PI)
-    tt("db", V("db", 1, 64), V("b2i", 0, 63), V("b2", 1, 64), ALU.subtract)
-
-    def scores(tag, t, bank, a, b, keep):
+    for t in range(R):
         for h in range(2):
-            mm("ms%s%d%d" % (tag, t, h), bank + h, "u2q", "u2s", 128 * h, "xq%d" % t, "xs%d" % t, a, b)
-            scale("cs%s%d%d" % (tag, t, h), V("w2%d" % t, L * h + keep, L * h + b),
-                  V("ps", 512 * (bank + h) + keep - a, 512 * (bank + h) + b - a), 1.0)
+            lin("b3%d%d" % (t, h), V("b3", 2 * t + h, 64, 4), V("b2", 32 * t + 16 * h, 32 * t + 16 * h + 16), 1.0, PI)
+    gather("bo", V("bo", 0, 32), V("b3", 0, 64), V("lu", 8, 10))
+    ts("bo2", V("bo", 32, 64), V("bo", 0, 32), SK, ALU.add, H128, ALU.subtract)
+    for side in range(2):
+        at = 120 * side
+        for k0, nk in RUNS:
+            for e in range(2):
+                a = 4 * (k0 - 1 + side)
+                lin("xx%d_%d_%d" % (side, k0, e), V("xx", at, at + 4 * nk), V("b3", a, a + 4 * nk), 1.0, 4.0 * e)
+                at += 4 * nk
+    for side in range(2):
+        gather("ot%d" % side, V("ot", 64 * side, 64 * side + 64), V("xx", 120 * side, 120 * side + 128),
+               V("lu", 4 * side, 4 * side + 4))
+    tt("db1", V("db", 0, 31), V("bo", 0, 31), V("bo", 1, 32), ALU.subtract)
+    lin("db", V("db", 0, 31), V("db", 0, 31), 1.0, PI)
 
-    scores("e", 0, 0, 0, C, 0)
+    def unpack(tag, t, banks, a, b, keep, end):
+        at = keep
+        for h in range(2):
+            k = banks[h]
+            mm("ms%s%d%d" % (tag, t, h), k, "u2q", "u2s", 128 * h, "xq%d" % t, "xs%d" % t, a, b)
+        for h in range(2):
+            k = banks[h]
+            scale("cs%s%d%d" % (tag, t, h), V("w2%d" % t, L * h + at, L * h + at + end - keep),
+                  V("ps", 512 * k + keep - a, 512 * k + end - a), 1.0)
+        for h in range(4):
+            k = banks[2 + h]
+            mm("md%s%d%d" % (tag, t, h), k, "eq", "es", 128 * h, "xq%d" % t, "xs%d" % t, a, b)
+            scale("cd%s%d%d" % (tag, t, h), V("dv%d" % t, PAD + L * h + at, PAD + L * h + at + end - keep),
+                  V("ps", 512 * k + keep - a, 512 * k + end - a), 0.5)
+
     for t in range(R):
         n = lambda s: "%s%d" % (s, t)
-        BW = V("b2i", 32 * t, 32 * t + 32)
-        gtt(n("otf"), V(n("otf"), 0, 128), BW, V("lu", 0, 8), V("e4", 0, 128), ALU.add)
-        copy(n("otc"), V(n("otc"), 0, 128), V(n("otf"), 0, 128))
-        gtt(n("kk"), V(n("kk"), 0, 64), V("b2", 32 * t, 32 * t + 32), V("lu", 24, 28), V("q4t", 0, 64), ALU.add)
-        copy(n("of0"), V(n("of0"), 0, 4), V(n("kk"), 0, 4))
-        for S in range(2):
-            gtt(n("pen%d" % S), V(n("pen"), 128 * S, 128 * S + 128), V("db", 32 * t, 32 * t + 32),
-                V("lu", 8 + 8 * S, 16 + 8 * S), V("ci", 0, 128), ALU.is_equal)
-            scale(n("pes%d" % S), V("a0", 512 * S + 1, 512 * S + 512, 4), V(n("pen"), 128 * S, 128 * S + 128), PEN)
-        if t == 0:
-            scores("l", 0, 2, L - 128, L, C)
-        else:
-            arrive("ax1", "xarr1", peers["from_next"], [V("xq1", C, L), V("xs1", C, L)], "sx1s")
-            scores("l", 1, 2, 128, L, 128)
-        for b in range(4):
-            mm(n("mdv%d" % b), 4 + b, "eq", "es", 128 * b, n("xq"), n("xs"), 0, L)
-            scale(n("cdv%d" % b), V(n("dv"), L * b, L * b + L), V("ps", 512 * (4 + b), 512 * (4 + b) + L), 0.5, "a")
-        DV = V(n("dv"), 0, 4 * L)
-        gather(n("n0"), V(n("nn"), 0, 64), DV, V(n("of0"), 0, 4), "a")
-        for S in range(2):
-            m = lambda s: "%s%s%d" % (s, "AB"[S], t)
+        gtt(n("kk"), V(n("kk"), 0, 128), V("bo", 32 + 16 * t, 48 + 16 * t), V("lu", 12, 20), V("q4t", 0, 128), ALU.add)
+        ts(n("pn0"), V(n("cf"), 0, 4), V(n("kk"), 0, 8, 2), H128, ALU.add, float(PAD), ALU.subtract)
+        lin(n("po0"), V(n("cf"), 4, 8), V(n("kk"), 0, 8, 2), 1.0, H128)
+        copy(n("of0"), V(n("off"), 0, 8), V(n("cf"), 0, 8))
+        scale(n("pp0"), V(n("po"), 0, 1), V(n("cf"), 4, 5), 1.0)
+        gtt(n("pen"), V(n("pen"), 0, 240), V("db", 16 * t, 16 * t + 16), V("lu", 20, 35), V("ci", 0, 240), ALU.is_equal)
+
+    unpack("o", 0, (0, 1, 2, 3, 4, 5), 0, C, 0, C)
+    unpack("r", 0, (6, 7, 0, 1, 2, 3), L - 128, L, C, L)
+    dma("ldv", "s", lambda: T.vb[:], lambda: T.v[:], 2200, [V("xs0", C, L)], [V("vb", 0, 512)], ["ldwc"])
+    quant("qv", "vq", "vs", 0, 128, V("vb", 0, 512))
+    for t in range(R):
+        n = lambda s: "%s%d" % (s, t)
+        state = V("lu", 10, 11)
+        scale(n("pes"), V("a0", 1, 960, 4), V(n("pen"), 0, 240), PEN)
+        for S, (k0, nk) in enumerate(RUNS):
+            m = lambda s: "%s%s%d" % (s, "ABCDEF"[S], t)
+            a, c, w, f = 64 * (k0 - 1), 16 * (k0 - 1), 16 * nk, 32 * t + 2 * (k0 - 1)
             for j in range(2):
-                a = 512 * S + 256 * j
-                gather(m("tg%d" % j), V(n("tg"), a, a + 256), V(n("w2"), 16, 2 * L), V(n("otc"), a // 16, a // 16 + 16), "va")
-                transpose(m("tb%d" % j), V(n("tb"), a, a + 256), V(n("tg"), a, a + 256))
-                gtt(m("dd%d" % j), V(n("dd"), a, a + 256), V(n("w2"), 0, 2 * L), V(n("otc"), 64 + a // 16, 80 + a // 16),
-                    V(n("tb"), a, a + 256), ALU.subtract)
-                for e in (2 * j, 2 * j + 1):
-                    o, i = V(n("ab"), 512 * S + e, 512 * S + 512, 4), V(n("dd"), 512 * S + 128 * e, 512 * S + 128 * e + 128)
-                    op(m("ab%d" % e), {"a": (lambda o=o, i=i: g.scalar.activation(ap(o), ap(i), ACT.Abs), ("n", 128))}, [i], [o])
-            a, c = 512 * S, 128 * S
-            scan(m("ms"), V(n("ms"), a + 4, a + 516), V("a0", a, a + 512), V(n("ab"), a, a + 512), ALU.add, ALU.max)
-            scan(m("mb"), V(n("mb"), c, c + 128), V(n("ms"), a + 3, a + 512, 4), V("rt", 0, 128), ALU.min, ALU.max)
-            tt(m("nf"), V(n("nf"), c, c + 128), V(n("ms"), a + 7, a + 516, 4), V(n("mb"), c, c + 128), ALU.is_ge)
-            scan(m("cn"), V(n("cn"), c, c + 128), V(n("nf"), c, c + 128), V("d1", 0, 128), ALU.mult, ALU.add, 0.5)
-            lin(m("fb"), V(n("fb"), c, c + 128), V(n("cn"), c, c + 128), 1.0, 16.0, "va", None, V("lu", 28, 36))
-            transpose(m("ft"), V(n("ft"), c, c + 128), V(n("fb"), c, c + 128))
-            for k in range(max(8 * S, 1), 8 * S + 8):
-                gather(n("st%d_" % k), V(n("sx"), 16 * k, 16 * k + 16), V(n("ft"), 16 * k, 16 * k + 16),
-                       V(n("sx"), 16 * k - 16, 16 * k - 15))
-            h = 32 * S
-            for lo, hi in STAGES[t]:
-                if lo // 8 == S:
-                    r = lambda s: "%s%d_%d" % (s, lo, t)
-                    copy(r("cf"), V(n("cf"), 4 * lo, 4 * hi), V(n("sx"), 16 * lo, 16 * hi, 4))
-                    tt(r("po"), V(n("po"), 4 * lo, 4 * hi), V(n("cf"), 4 * lo, 4 * hi), V(n("kk"), 4 * lo, 4 * hi), ALU.add)
-                    copy(r("off"), V(n("off"), 4 * lo, 4 * hi), V(n("po"), 4 * lo, 4 * hi))
-            for j in range(2):
-                f, w = h + 16 * j, min(16, 60 - h - 16 * j)
-                gather(m("nn%d" % j), V(n("nn"), 16 * f + 64, 16 * (f + w) + 64), V(n("dv"), 16, 4 * L), V(n("off"), f, f + w), "a")
-                gtt(m("zt%d" % j), V(n("zt"), 16 * f, 16 * f + 256), DV, V(n("off"), f, f + 16),
-                    V(n("nn"), 16 * f, 16 * f + 256), ALU.add)
-            quant(m("qz"), n("zq"), n("zs"), c, c + 128, V(n("zt"), a, a + 512))
-        scale(n("pos"), V("pos", 16 * t, 16 * t + 16), V(n("po"), 0, 64, 4), 1.0)
+                x, y = a + 2 * w * j, a + 2 * w * (j + 1)
+                gather(m("tg%d" % j), V(n("tg"), x, y), V(n("w2"), 16 + 8 * j, 2 * L), V("ot", f, f + 2 * nk), "va")
+                transpose(m("tb%d" % j), V(n("tb"), x, y), V(n("tg"), x, y))
+                gtt(m("dd%d" % j), V(n("dd"), x, y), V(n("w2"), 8 * j, 2 * L), V("ot", 64 + f, 64 + f + 2 * nk),
+                    V(n("tb"), x, y), ALU.subtract)
+            for e in range(4):
+                o, i = V(n("ab"), a + e, a + 4 * w, 4), V(n("dd"), a + w * e, a + w * e + w)
+                op(m("ab%d" % e), {"a": (lambda o=o, i=i: g.scalar.activation(ap(o), ap(i), ACT.Abs), ("n", w))}, [i], [o])
+            scan(m("ms"), V("ms", a + 4, a + 4 * w + 4), V("a0", a, a + 4 * w), V(n("ab"), a, a + 4 * w), ALU.add, ALU.max)
+            scan(m("mb"), V(n("mb"), c, c + w), V("ms", a + 3, a + 4 * w, 4), V("rt", 0, w), ALU.min, ALU.max)
+            tt(m("nf"), V(n("nf"), c, c + w), V("ms", a + 7, a + 4 * w + 4, 4), V(n("mb"), c, c + w), ALU.is_ge)
+            scan(m("cn"), V(n("cn"), c, c + w), V(n("nf"), c, c + w), V("d1", c, c + w), ALU.mult, ALU.add)
+            copy(m("fu"), V(n("fu"), 8 * S, 8 * S + nk), V(n("cn"), c + 15, c + w, 16))
+            tb, ng = 2 * PAIRS * S, nk - 1 - nk % 2
+            gather(m("ft"), V("tt", tb, tb + w), V("idt", 0, 144), V(n("fu"), 8 * S, 8 * S + nk), "va")
+            gather(m("gg"), V("tt", tb + PAIRS, tb + PAIRS + 16 * ng), V("tt", tb, tb + w), V(n("fu"), 8 * S, 8 * S + ng), "va")
+            table = V("tt", tb, tb + PAIRS + 16 * (ng + 2 * (nk % 2)))
+            for k in range(k0, k0 + nk, 2):
+                if k in DIRECT:
+                    gtt(n("po%d_" % k), V(n("po"), 8 * k, 8 * k + 16), table, state, V(n("kk"), 8 * k, 8 * k + 16), ALU.add)
+                else:
+                    gather(n("cg%d_" % k), V(n("cg"), 8 * k, 8 * k + 16), table, state, "a")
+                if k + 2 < 16:
+                    gather(n("st%d_" % k), V(n("sx"), 16 * k, 16 * k + 16), table, state)
+                    state = V(n("sx"), 16 * k + (8 if k + 1 < k0 + nk else 0), 16 * k + (9 if k + 1 < k0 + nk else 1))
+        for lo, hi in PLACES[t]:
+            if lo not in DIRECT:
+                tt(n("pt%d_" % lo), V(n("po"), 8 * lo, 8 * hi, 2), V(n("cg"), 8 * lo, 8 * hi, 2), V(n("kk"), 8 * lo, 8 * hi, 2), ALU.add)
+            copy(n("off%d_" % lo), V(n("off"), 4 * lo + 4, 4 * hi + 4), V(n("po"), 8 * lo, 8 * hi, 2))
+        for lo, hi in TEMPLATES[t]:
+            gather(n("nn%d_" % lo), V(n("nn"), 64 * lo, 64 * hi), V(n("dv"), 16, PAD + 4 * L), V(n("off"), 4 * lo, 4 * hi), "va")
+        lin(n("pos"), V("pos", 16 * t, 16 * t + 16), V(n("po"), 0, 128, 8), 1.0, -float(PAD))
         if t == 1:
-            arrive("aw1", "warr1", peers["from_w1"], [V("wq1", 0, 512), V("wp1", 0, 512)], "sx1s")
+            arrive("aw1", "warr1", peers["from_w1"], [V("wq1", 0, 512), V("wp1", 0, 512)], "swfs")
         nq, ns = "xq%d" % (t + 1), "xs%d" % (t + 1)
-        for S in range(2):
+        for S, (c, d) in enumerate(((0, CUT[t]), (CUT[t], C))):
             m = lambda s: "%s%s%d" % (s, "AB"[S], t)
-            a, c = 512 * S, 128 * S
+            a, z = (0, max(d, 128)) if S == 0 else (min(c, C - 128), C)
+            if z > d:
+                for name in ("zt", "ht", "xt"):
+                    memset(m("m_" + name), V(n(name), 4 * d, 4 * z), 0.0)
+            for lo, hi in SUMS[t]:
+                if c <= 16 * lo < d:
+                    gtt(n("zt%d_" % lo), V(n("zt"), 64 * lo, 64 * hi), V(n("dv"), 0, PAD + 4 * L),
+                        V(n("off"), 4 * lo + 4, 4 * hi + 4), V(n("nn"), 64 * lo, 64 * hi), ALU.add)
+            quant(m("qz"), n("zq"), n("zs"), a, z, V(n("zt"), 4 * a, 4 * z))
             for b in range(4):
                 k = 4 * S + b
-                mm(m("mr%d" % b), k, n("wq"), n("wp"), 128 * b, n("zq"), n("zs"), c, c + 128)
-                scale(m("ch%d" % b), V(n("ht"), a + b, a + 512, 4), V("ps", 512 * k, 512 * k + 128), 0.03125)
-            quant(m("qh"), n("hq"), n("hs"), c, c + 128, V(n("ht"), a, a + 512))
+                mm(m("mr%d" % b), k, n("wq"), n("wp"), 128 * b, n("zq"), n("zs"), a, z)
+                scale(m("ch%d" % b), V(n("ht"), 4 * c + b, 4 * d, 4), V("ps", 512 * k + c - a, 512 * k + d - a), 0.03125)
+            quant(m("qh"), n("hq"), n("hs"), a, z, V(n("ht"), 4 * a, 4 * z))
             for b in range(4):
                 k = 4 * S + b
-                mm(m("mz%d" % b), k, "eq", "es", 128 * b, n("zq"), n("zs"), c, c + 128, True, False)
-                mm(m("mh%d" % b), k, "eq", "es", 128 * b, n("hq"), n("hs"), c, c + 128, False, True, m("mz%d" % b))
-                scale(m("cx%d" % b), V(n("xt"), a + b, a + 512, 4), V("ps", 512 * k, 512 * k + 128), 1.0)
-            quant(m("qx"), nq, ns, c, c + 128, V(n("xt"), a, a + 512))
-            if S == 0 and t == 0:
-                scores("e", 1, 0, 0, 128, 0)
-            if S == 0 and t == 1:
-                mm("myA", 0, "vq", "vs", 0, nq, ns, 0, 128)
-                scale("cyA", V("yb", 0, 128), V("ps", 0, 128), 1.0)
-            if S == 0 and t == 0:
+                mm(m("mz%d" % b), k, "eq", "es", 128 * b, n("zq"), n("zs"), a, z, True, False)
+                mm(m("mh%d" % b), k, "eq", "es", 128 * b, n("hq"), n("hs"), a, z, False, True, m("mz%d" % b))
+                scale(m("cx%d" % b), V(n("xt"), 4 * c + b, 4 * d, 4), V("ps", 512 * k + c - a, 512 * k + d - a), 1.0)
+            quant(m("qx"), nq, ns, a, z, V(n("xt"), 4 * a, 4 * z))
+            if t == 0 and S == 0:
                 ship("sx1", peers["prev"], "xarr1", "xq1", "xs1", C, "xq1", "xs1", 0, B)
                 ship("swf", peers["prev"] if peers["forward"] else None, "warr1", "wq1", "wp1", 0, "wq0", "wp0", 0, 512)
-    mm("myB", 1, "vq", "vs", 0, "xq2", "xs2", 128, 256)
-    scale("cyB", V("yb", 128, 256), V("ps", 512, 640), 1.0)
+                arrive("ax1", "xarr1", peers["from_next"], [V("xq1", C, L), V("xs1", C, L)], "sx1s")
+                unpack("a", 1, (0, 1, 2, 3, 0, 1), a, z, c, d)
+            if t == 0 and S == 1:
+                unpack("b", 1, (0, 1, 2, 3, 4, 5), c, L, c, L)
+            if t == 1:
+                mm(m("my"), 4 * S, "vq", "vs", 0, nq, ns, a, z)
+                scale(m("cy"), V("yb", c, d), V("ps", 2048 * S + c - a, 2048 * S + d - a), 1.0)
 
     dma("ool", "s", lambda: T.ol[:], lambda: T.pos[0:128:16, :], 1, [V("pos", 0, 32)], [])
-    for S in range(2):
-        c = 128 * S
-        dma("ooc%d" % S, "sa", lambda c=c: T.oc[:, 4 * c:4 * c + 512], lambda c=c: T.xq2[:, c:c + 128].bitcast(dt.uint8), 64,
-            [V("xq2", c, c + 128)], [])
-        dma("oy%d" % S, "sa", lambda c=c: T.y[:, c:c + 128], lambda c=c: T.yb[:, c:c + 128], 64, [V("yb", c, c + 128)], [])
+    cut = min(CUT[1], C - 128)
+    for S, (c, d, e, f) in enumerate(((0, cut, 0, CUT[1]), (cut, C, CUT[1], C))):
+        dma("ooc%d" % S, "sa", lambda c=c, d=d: T.oc[:, 4 * c:4 * d],
+            lambda c=c, d=d: T.xq2[:, c:d].bitcast(dt.uint8), (d - c) / 2, [V("xq2", c, d)], [])
+        dma("oy%d" % S, "sa", lambda e=e, f=f: T.y[:, e:f], lambda e=e, f=f: T.yb[:, e:f], (f - e) / 2, [V("yb", e, f)], [])
     for k in range(4):
-        dma("osc%d" % k, "sa", lambda k=k: T.osc[4 * k:4 * k + 4, :], lambda k=k: T.xs2[32 * k:32 * k + 4, :], 1,
+        dma("osc%d" % k, "sa", lambda k=k: T.osc[4 * k:4 * k + 4, :], lambda k=k: T.xs2[32 * k:32 * k + 4, 0:C], 1,
             [V("xs2", 0, C)], [])
     return ops
 
@@ -388,6 +437,136 @@ def depend(ops):
     return index
 
 
+PLAN = {"cycle": 1.04, "gather": 1.62, "tensor": 0.7, "scalar": 15.0, "hand": 105.0, "dma": 1800.0, "kb": 5.0, "remote": 3100.0,
+        "first": 500.0, "layer": 4500.0, "seed": 1, "turns": 40000, "allow": 100.0, "early": 1.0, "reach": 800.0}
+
+
+def times(cost, first, q):
+    kind, n = cost
+    if kind == "dma":
+        return 60.0, PLAN["dma"] + PLAN["kb"] * n
+    if kind == "rem":
+        return 300.0 + (PLAN["first"] if first else 0.0), 0.0
+    if kind == "arr":
+        return 0.0, PLAN["remote"] + n
+    t = {"n": PLAN["cycle"] * (max(64, n) if q == "v" else PLAN["scalar"] + n), "gv": 62 + PLAN["gather"] * n, "ga": 81 + PLAN["gather"] * n,
+         "q": 15 + 0.275 * n, "mm": PLAN["tensor"] * (n + 16), "io": 160 + 2 * PLAN["cycle"] * n}[kind]
+    return t, t
+
+
+def plan(ops):
+    n = len(ops)
+    first = [i for i in range(n) if ops[i]["kind"] in ("rem", "none")][0]
+    tm = [{q: times(a[1], i == first, q) for q, a in o["alts"].items()} for i, o in enumerate(ops)]
+    users = [[] for _ in ops]
+    for i, o in enumerate(ops):
+        for d in o["dep"] | o["aft"]:
+            users[d].append(i)
+    rank = [None] * n
+
+    def way(i):
+        if rank[i] is None:
+            rank[i] = max(min(tm[i].values())) + max([way(u) + PLAN["hand"] for u in users[i]] + [0.0])
+        return rank[i]
+
+    for i in reversed(range(n)):
+        way(i)
+    hand = PLAN["hand"]
+    dep, aft = [list(o["dep"]) for o in ops], [list(o["aft"]) for o in ops]
+    needs = [dep[i] + aft[i] for i in range(n)]
+    either = ["v" in tm[i] and "a" in tm[i] for i in range(n)]
+
+    def place(prio, force):
+        starts, ends = {q: [] for q in "vapsgx"}, {q: [] for q in "vapsgx"}
+        at, fin, end, queue = [0.0] * n, [0.0] * n, [0.0] * n, [None] * n
+        for i in sorted(range(n), key=lambda i: -prio[i]):
+            r = max([fin[d] + hand for d in dep[i]] + [end[d] for d in aft[i]] + [0.0])
+            best = None
+            for q, (hold, lat) in tm[i].items():
+                if force[i] in (None, q):
+                    s, a, b = r, starts[q], ends[q]
+                    k = len(b)
+                    while k and b[k - 1] > s:
+                        k -= 1
+                    while k < len(a) and s + hold > a[k]:
+                        s = max(s, b[k])
+                        k += 1
+                    if best is None or s + lat < best[0]:
+                        best = (s + lat, s, q, k)
+            fin[i], at[i], q, k = best
+            end[i], queue[i] = at[i] + tm[i][q][0], q
+            if q != "x":
+                starts[q].insert(k, at[i])
+                ends[q].insert(k, end[i])
+        return max(fin), at, fin, end, queue
+
+    def tight(p):
+        total, at, fin, end, queue = p
+        ahead = {(queue[i], end[i]): i for i in range(n)}
+        i, calls, pairs = fin.index(total), [], []
+        while i is not None:
+            calls.append(i)
+            c = [d for d in dep[i] if fin[d] + hand == at[i]] + [d for d in aft[i] if end[d] == at[i]]
+            before = c[0] if c else ahead.get((queue[i], at[i]))
+            if before is not None and not c:
+                pairs.append((before, i))
+            i = before
+        return calls, pairs
+
+    def move(prio, i, to):
+        up = to > prio[i]
+        prio[i], todo = to, [i]
+        while todo:
+            x = todo.pop()
+            for d in (needs[x] if up else users[x]):
+                if (prio[d] <= prio[x]) if up else (prio[d] >= prio[x]):
+                    prio[d] = prio[x] + (0.001 if up else -0.001)
+                    todo.append(d)
+
+    seed = [PLAN["seed"]]
+
+    def draw():
+        seed[0] = (seed[0] * 6364136223846793005 + 1442695040888963407) % 2 ** 64
+        return (seed[0] >> 11) / 2.0 ** 53
+
+    def worth(p):
+        return p[0] + PLAN["early"] * sum(p[1]) / n
+
+    now = best = place(rank, [None] * n)
+    calls, pairs = tight(now)
+    for turn in range(PLAN["turns"]):
+        p, f, r = [-now[1][i] - 0.0001 * i for i in range(n)], list(now[4]), draw()
+        if r < 0.6 and pairs:
+            u, v = pairs[int(draw() * len(pairs))]
+            x = u if draw() < 0.5 else v
+            if r < 0.18 and either[x]:
+                f[x] = "a" if f[x] == "v" else "v"
+            elif x == v:
+                move(p, v, p[u] + 1 + PLAN["reach"] * draw() ** 2)
+            else:
+                move(p, u, p[v] - 1 - 2 * PLAN["reach"] * draw() ** 2)
+        elif r < 0.75:
+            x = calls[int(draw() * len(calls))]
+            move(p, x, p[x] + PLAN["reach"] * draw())
+        else:
+            x = int(draw() * n)
+            if r < 0.85 and either[x]:
+                f[x] = "a" if f[x] == "v" else "v"
+            else:
+                move(p, x, p[x] + 2 * PLAN["reach"] * (draw() - draw()))
+        e = place(p, f)
+        if worth(e) <= worth(now) - PLAN["allow"] * math.log(1 - draw()) * (1 - turn / PLAN["turns"]):
+            now = e
+            calls, pairs = tight(now)
+            if worth(e) < worth(best):
+                best = e
+    PLANNED.append(best)
+    return [(i, best[4][i]) for i in sorted(range(n), key=lambda i: (best[1][i], i)) if best[4][i] != "x"]
+
+
+PLANNED, ORDER = [], []
+
+
 def emit(g, T, ops, order):
     queues = {"v": g.vector, "a": g.scalar, "p": g.tensor, "s": g.sync, "g": g}
     known = {q: set() for q in queues}
@@ -409,7 +588,7 @@ def emit(g, T, ops, order):
     last, count, mark = [None] * NPOOL, [0] * NPOOL, {}
     for i, o in enumerate(ops):
         if o["kind"] == "ext":
-            mark[i] = o["ext"][:2]
+            mark[i] = o["ext"]
     sent = 0
     for i, q in order:
         for d in waits[i]:
@@ -446,8 +625,13 @@ def wiring(T, topo, rank):
     def relayed(q):
         return together(q, q + 1) and not together(q, q + 2)
 
+    def helped(q):
+        return relayed(q) and not together(q, q - 1)
+
     return {"prev": peer(rank - 1), "direct": None if relayed(rank - 2) else peer(rank - 2), "forward": relayed(rank - 1),
-            "from_next": 2 * len(engines(rank + 1, rank)),
+            "helper": peer(rank + 1) if helped(rank) else None,
+            "from_next": 2 * len(engines(rank + 1, rank)), "from_prev": 2 * len(engines(rank - 1, rank)),
+            "from_w0": 2 * len(engines(rank + 1, rank)) + (2 * len(engines(rank + 2, rank)) if helped(rank + 1) else 0),
             "from_w1": 2 * len(engines(rank + (1 if relayed(rank) else 2), rank))}
 
 
@@ -457,5 +641,6 @@ def rank_program(g, core, T, topo):
         return
     ops = program(g, T, wiring(T, topo, rank))
     depend(ops)
-    order = [(int(w[:-1], 16), w[-1]) for w in ORDER.split()]
-    emit(g, T, ops, [e for e in order if ops[e[0]]["kind"] != "none"])
+    if not ORDER:
+        ORDER.extend(plan(ops))
+    emit(g, T, ops, [e for e in ORDER if ops[e[0]]["kind"] != "none"])

import math

from concourse.mybir import dt, AluOpType, ActivationFunctionType

ALU = AluOpType
ACT = ActivationFunctionType
C, B, L, R = 256, 96, 352, 2
Q4, U8, F32, BF, I32, U16 = "float8_e4m3fn_x4", "uint8", "float32", "bfloat16", "int32", "uint16"
PAD = 16
RUNS = ((1, 5), (6, 4), (10, 6))
PLACES = (((1, 4), (4, 6), (6, 10), (10, 14), (14, 16)),) * 2
TEMPLATES = (((0, 5), (5, 7), (7, 11), (11, 15), (15, 16)),) * 2
SUMS = (((0, 4), (4, 6), (6, 10), (10, 14), (14, 16)), ((0, 4), (4, 8), (8, 12), (12, 14), (14, 16)))
DIRECT = tuple(range(16))
OWN = 336
CUT = (96, 128)
PAIRS = 16 * max(_r[1] for _r in RUNS)

SCRATCH = {
    "ps": ("psum", [128, 4096], F32),
    "xb": ("sbuf", [128, 4 * C], BF), "ub": ("sbuf", [128, 512], BF), "vb": ("sbuf", [128, 512], BF),
    "sti": ("sbuf", [128, 2], I32), "stf": ("sbuf", [128, 4], F32),
    "uq": ("sbuf", [128, 128], Q4), "us": ("sbuf", [128, 128], U8),
    "u2q": ("sbuf", [128, 256], Q4), "u2s": ("sbuf", [128, 256], U8),
    "vq": ("sbuf", [128, 128], Q4), "vs": ("sbuf", [128, 128], U8),
    "woq": ("sbuf", [128, 512], Q4), "wos": ("sbuf", [128, 512], U8),
    "hq": ("sbuf", [128, 512 - OWN], Q4), "hs": ("sbuf", [128, 512 - OWN], U8),
    "et": ("sbuf", [128, 516], BF), "eq": ("sbuf", [128, 512], Q4), "es": ("sbuf", [128, 512], U8),
    "pi": ("sbuf", [128, 8], I32), "pf": ("sbuf", [128, 16], F32),
    "xf": ("sbuf", [128, 144], F32), "idt": ("sbuf", [128, 144], F32), "ci": ("sbuf", [128, 240], F32),
    "yy": ("sbuf", [128, 4], F32), "q4t": ("sbuf", [128, 128], F32),
    "lf": ("sbuf", [128, 20], F32), "lu": ("sbuf", [128, 36], U16),
    "xx": ("sbuf", [128, 248], F32), "ot": ("sbuf", [128, 128], U16),
    "ms": ("sbuf", [128, 964], F32), "tt": ("sbuf", [128, 2 * PAIRS * len(RUNS)], F32),
    "upf": ("sbuf", [128, 16], I32), "upu": ("sbuf", [128, 16], U16),
    "bi": ("sbuf", [128, 64], F32), "b2": ("sbuf", [128, 64], F32), "b3": ("sbuf", [128, 64], F32),
    "bo": ("sbuf", [128, 64], F32), "db": ("sbuf", [128, 32], F32),
    "a0": ("sbuf", [128, 960], BF), "rt": ("sbuf", [128, 128], F32), "d1": ("sbuf", [128, 240], F32),
    "pos": ("sbuf", [128, 32], F32), "yb": ("sbuf", [128, C], F32),
    "xq2": ("sbuf", [128, L], Q4), "xs2": ("sbuf", [128, L], U8),
}
for _t in range(R):
    for _n, _w, _d in (("xq", L, Q4), ("xs", L, U8), ("wq", 512, Q4), ("wp", 512, U8), ("w2", 2 * L, F32),
                       ("kk", 136, F32), ("cg", 136, F32), ("pen", 240, F32),
                       ("tg", 960, F32), ("tb", 960, F32), ("dd", 960, F32), ("ab", 960, F32),
                       ("mb", 240, F32), ("nf", 240, F32), ("cn", 240, F32), ("fu", 48, U16),
                       ("sx", 256, U16), ("cf", 8, F32), ("po", 136, F32),
                       ("off", 68, U16),
                       ("dv", PAD + 4 * L, F32), ("nn", 1024, F32), ("zt", 1024, BF), ("zq", C, Q4), ("zs", C, U8),
                       ("ht", 1024, BF), ("hq", C, Q4), ("hs", C, U8), ("xt", 1024, BF)):
        SCRATCH["%s%d" % (_n, _t)] = ("sbuf", [128, _w], _d)
NPOOL = 140
SEMAPHORES = ["s%d" % _i for _i in range(NPOOL)] + ["sent", "xarr0", "xarr1", "warr0", "warr1", "hop"]
HUGE, PEN = 2.0 ** 92, 2.0 ** 88


def span(v):
    n, a, b, s = v
    if n == "ps":
        a, b, s = a // 512, a // 512 + 1, 1
    m = 0
    if s == 1:
        return ((1 << (b - a)) - 1) << a
    for j in range(a, b, s):
        m |= 1 << j
    return m


def program(g, T, peers):
    ops = []

    def V(n, a, b, s=1):
        return (n, a, b, s)

    def ap(v):
        n, a, b, s = v
        return T[n][:, a:b] if s == 1 else T[n][:, a:b:s]

    def width(v):
        return len(range(v[1], v[2], v[3]))

    def op(name, alts, rd, wr, acc=None, after=(), ext=None, kind="c"):
        ops.append({"name": name, "alts": alts, "rd": rd, "wr": wr, "acc": acc, "after": list(after), "ext": ext,
                    "kind": kind})

    def vec(name, fn, cost, rd, wr):
        op(name, {"v": (fn, cost)}, rd, wr)

    def sc(x):
        return ap(x) if isinstance(x, tuple) else x

    def aps(*xs):
        return [x for x in xs if isinstance(x, tuple)]

    def memset(name, o, val):
        f = 0.5 if SCRATCH[o[0]][2] in (BF, U16) else 1
        alts = {"v": (lambda: g.vector.memset(ap(o), val), ("n", width(o) * f))}
        row = V("xf" if width(o) <= 144 else "ci", 0, width(o))
        if width(o) <= 240:
            alts["a"] = (lambda: g.scalar.activation(ap(o), ap(row), ACT.Identity, bias=val, scale=0.0), ("n", width(o)))
        op(name, alts, [row] if "a" in alts else [], [o])

    def copy(name, o, i):
        vec(name, lambda: g.vector.tensor_copy(ap(o), ap(i)), ("n", width(o)), [i], [o])

    def tt(name, o, a, b, alu):
        vec(name, lambda: g.vector.tensor_tensor(ap(o), ap(a), ap(b), alu), ("n", 2 * width(o)), [a, b], [o])

    def ts(name, o, i, s1, op0, s2=None, op1=None):
        if op1 is None:
            fn = lambda: g.vector.tensor_scalar(ap(o), ap(i), sc(s1), None, op0)
        else:
            fn = lambda: g.vector.tensor_scalar(ap(o), ap(i), sc(s1), sc(s2), op0, op1)
        vec(name, fn, ("n", width(o)), [i] + aps(s1, s2), [o])

    def gtt(name, o, win, off, b, alu):
        vec(name, lambda: g.vector.tensor_tensor(ap(o), ap(win).indirect(ap(off)), ap(b), alu), ("gv", width(o)),
            [win, off, b], [o])

    def gather(name, o, win, off, queues="v"):
        alts = {}
        if "v" in queues:
            alts["v"] = (lambda: g.vector.tensor_copy(ap(o), ap(win).indirect(ap(off))), ("gv", width(o)))
        if "a" in queues:
            alts["a"] = (lambda: g.scalar.activation(ap(o), ap(win).indirect(ap(off)), ACT.Copy), ("ga", width(o)))
        op(name, alts, [win, off], [o])

    def scale(name, o, i, k, queues="va"):
        alts = {}
        if "v" in queues:
            if k == 1.0:
                alts["v"] = (lambda: g.vector.tensor_copy(ap(o), ap(i)), ("n", width(o)))
            else:
                alts["v"] = (lambda: g.vector.tensor_scalar(ap(o), ap(i), k, None, ALU.mult), ("n", width(o)))
        if "a" in queues:
            alts["a"] = (lambda: g.scalar.activation(ap(o), ap(i), ACT.Copy, scale=k), ("n", width(o)))
        psum = [i] if i[0] == "ps" else []
        op(name, alts, [] if psum else [i], [o] + psum)

    def lin(name, o, i, k, bias, queues="va"):
        alts = {}
        if "v" in queues:
            alts["v"] = (lambda: g.vector.tensor_scalar(ap(o), ap(i), k, sc(bias), ALU.mult, ALU.add), ("n", width(o)))
        if "a" in queues:
            alts["a"] = (lambda: g.scalar.activation(ap(o), ap(i), ACT.Identity, bias=sc(bias), scale=k), ("n", width(o)))
        op(name, alts, [i] + aps(bias), [o])

    def scan(name, o, d0, d1, op0, op1):
        vec(name, lambda: g.vector.tensor_tensor_scan(ap(o), ap(d0), ap(d1), 0.0, op0, op1), ("n", width(o)),
            [d0, d1], [o])

    def transpose(name, o, i):
        vec(name, lambda: g.vector.transpose(ap(o), ap(i)), ("n", width(o)), [i], [o])

    def quant(name, q, s, a, b, i):
        o, p = V(q, a, b), V(s, a, b)
        vec(name, lambda: g.vector.quantize_mx(ap(o), ap(p), ap(i)), ("q", width(i)), [i], [o, p])

    def mm(name, bank, lq, ls, la, rq, rs, ra, rb, start=True, stop=True, acc=None):
        o = V("ps", 512 * bank, 512 * bank + rb - ra)
        a, b, c, d = V(lq, la, la + 128), V(ls, la, la + 128), V(rq, ra, rb), V(rs, ra, rb)
        op(name, {"p": (lambda: g.tensor.matmul_mx(ap(o), ap(a), ap(b), ap(c), ap(d), start, stop), ("mm", rb - ra))},
           [a, b, c, d], [o], acc=acc)

    def iota(name, o, pattern, base, cm, after=()):
        if SCRATCH[o[0]][2] == I32:
            fn = lambda: g.iota(ap(o), pattern, base, cm)
        else:
            fn = lambda: g.iota(ap(o), pattern, base, cm, allow_small_or_imprecise_dtypes=True)
        op(name, {"g": (fn, ("io", width(o)))}, [], [o], after=after)

    def dma(name, queues, dst, src, kb, rd, wr, after=()):
        alts = {}
        if "s" in queues:
            alts["s"] = (lambda: g.sync.dma_start(dst(), src()), ("dma", kb))
        if "a" in queues:
            alts["a"] = (lambda: g.scalar.dma_start(dst(), src()), ("dma", kb))
        op(name, alts, rd, wr, after=after, kind="dma")

    def codes(v):
        return ap(v).bitcast(dt.uint8)

    last_remote = []

    def ship(name, peer, sem, dq, ds, da, sq, ss, sa, n, scales_first=False):
        a, b, c, d = V(dq, da, da + n), V(sq, sa, sa + n), V(ds, da, da + n), V(ss, sa, sa + n)
        sems = sem if scales_first else (sem, sem)
        calls = [("c", b, lambda: g.remote_dma(codes(a), codes(b), T.sem[sems[1]], T.sem["sent"], peer[1], peer[0], peer[2])),
                 ("s", d, lambda: g.remote_dma(ap(c), ap(d), T.sem[sems[0]], T.sem["sent"], peer[1], peer[0], peer[2]))]
        for tag, src, fn in (calls[::-1] if scales_first else calls):
            op(name + tag, {"g": (fn, ("rem", 0))}, [src], [], after=last_remote[-1:], kind="none" if peer is None else "rem")
            ops[-1]["eng"] = 0 if peer is None else peer[3]
            last_remote.append(name + tag)

    def arrive(name, sem, count, wr, like, more=0.0):
        op(name, {"x": (None, ("arr", more))}, [], wr, after=[like], ext=(sem, count), kind="ext")

    dma("ldxA", "s", lambda: T.xb[:, 0:512], lambda: T.x[:, 0:512], 128, [], [V("xb", 0, 512)])
    dma("ldst", "a", lambda: T.sti[:], lambda: T.st[:], 8, [], [V("sti", 0, 2)])
    dma("ldu", "a", lambda: T.ub[:], lambda: T.u[:], 256, [], [V("ub", 0, 512)], ["ldst"])
    dma("ldwd", "s", lambda: T.woq[:, OWN:512].bitcast(dt.uint8), lambda: T.wc[:, 4 * OWN:2048], 340, [],
        [V("woq", OWN, 512)], ["ldxA"])
    dma("ldws", "s", lambda: T.wos[:], lambda: T.ws[:], 410, [], [V("wos", 0, 512)], ["ldwd"])
    dma("ldxB", "a", lambda: T.xb[:, 512:1024], lambda: T.x[:, 512:1024], 540, [], [V("xb", 512, 1024)], ["ldu"])
    dma("ldwc", "s", lambda: T.woq[:, 0:OWN].bitcast(dt.uint8), lambda: T.wc[:, 0:4 * OWN], 700, [], [V("woq", 0, OWN)], ["ldws"])

    iota("ipi", V("pi", 0, 1), [[0, 1]], 0, 1)
    iota("ixf", V("xf", 0, 144), [[1, 144]], 0, 0, ["ipi"])
    iota("iup", V("upf", 0, 16), [[16, 2], [32, 4], [0, 2]], 0, 0, ["ixf"])
    iota("iyy", V("yy", 0, 4), [[2, 2], [64, 2]], 0, 0, ["iup"])
    quant("qxA", "xq0", "xs0", 0, 128, V("xb", 0, 512))
    quant("qxB", "xq0", "xs0", 128, C, V("xb", 512, 1024))
    iota("ici", V("ci", 0, 240), [[0, 15], [1, 16]], -16, 0, ["iyy"])
    last_remote.append("ici")
    ship("sx0", peers["prev"], "xarr0", "xq0", "xs0", C, "xq0", "xs0", 0, B)
    ship("swh", peers["helper"], "hop", "hq", "hs", 0, "woq", "wos", OWN, 512 - OWN)
    ship("sw0", peers["prev"], "warr0", "wq0", "wp0", 0, "woq", "wos", 0, 512 if peers["helper"] is None else OWN)
    arrive("ax0", "xarr0", peers["from_next"], [V("xq0", C, L), V("xs0", C, L)], "sx0s")
    arrive("aw0", "warr0", peers["from_w0"], [V("wq0", 0, 512), V("wp0", 0, 512)], "sw0s", PLAN["layer"])
    arrive("ah", "hop", peers["from_prev"], [V("hq", 0, 512 - OWN), V("hs", 0, 512 - OWN)], "swhs")
    for k0, nk in RUNS + ((16, 1),):
        iota("iq%d" % k0, V("q4t", 8 * k0 - 8, 8 * (k0 + nk) - 8), [[-16, nk], [4, 4], [0, 2]], PAD, 0, ["sw0s"])
        last_remote.append("iq%d" % k0)
    ship("swo", peers["direct"], "warr0", "wq0", "wp0", OWN, "hq", "hs", 0, 512 - OWN)
    ship("swd", peers["direct"], "warr1", "wq1", "wp1", 0, "woq", "wos", 0, 512)

    for j, (shift, mask) in enumerate(((0, 15), (4, 1), (3, 1), (0, 3), (2, 3), (0, 1))):
        ts("pi%d" % j, V("pi", 1 + j, 2 + j), V("pi", 0, 1), shift, ALU.logical_shift_right, mask, ALU.bitwise_and)
    copy("pf", V("pf", 0, 7), V("pi", 0, 7))
    P, PI, GP, HI, P4, PQ, ODD, GL, H128, LB, LA, SK = [V("pf", j, j + 1) for j in range(12)]
    lin("gl", GL, GP, float(L), 0.0)
    lin("h128", H128, HI, float(PAIRS), 0.0)
    lin("lb", LB, PI, 4.0, GP)
    ts("la1", V("pf", 13, 14), GP, ODD, ALU.subtract, 3.0, ALU.mult)
    lin("la", LA, V("pf", 13, 14), 1.0, LB)
    lin("sk1", V("pf", 12, 13), P4, float(L), PQ)
    ts("sk", SK, V("pf", 12, 13), PI, ALU.subtract, GL, ALU.subtract)
    lin("lfa", V("lf", 0, 4), V("yy", 0, 4), 1.0, LA)
    lin("lfb", V("lf", 4, 8), V("yy", 0, 4), 1.0, LB)
    lin("lfo", V("lf", 8, 10), V("xf", 0, 2), 2.0, LB)
    lin("lfh", V("lf", 10, 12), V("xf", 0, 2), 0.0, H128)
    lin("lfq", V("lf", 12, 20), V("xf", 0, 8), 2.0, HI)
    copy("lu", V("lu", 0, 20), V("lf", 0, 20))
    copy("luk", V("lu", 20, 36), V("xf", 0, 16))
    copy("upu", V("upu", 0, 16), V("upf", 0, 16))
    lin("idt", V("idt", 0, 144), V("xf", 0, 144), 1.0, H128)
    memset("m_et", V("et", 0, 516), 0.0)
    ts("et", V("et", 3, 515, 4), V("xf", 0, 128), P, ALU.is_equal)
    for b in range(4):
        quant("qe%d" % b, "eq", "es", 128 * b, 128 * b + 128, V("et", 3 - b, 515 - b))
    for e, val in ((0, -HUGE), (2, 0.0), (3, 0.0)):
        memset("m_a%d" % e, V("a0", e, 960, 4), val)
    memset("m_rt", V("rt", 0, 128), 0.0)
    memset("m_rt0", V("rt", 0, 128, 16), HUGE)
    memset("m_d1", V("d1", 0, 240), -1.0)
    memset("m_d15", V("d1", 15, 240, 16), 15.0)
    for S, (k0, nk) in enumerate(RUNS):
        lin("d1_%d" % k0, V("d1", 16 * k0 - 1, 16 * (k0 + nk - 2), 16), V("xf", 16, 16 * nk, 16), 1.0, 15.0)
        tb = 2 * PAIRS * S
        if 16 * nk < PAIRS:
            memset("m_ta%d" % S, V("tt", tb + 16 * nk, tb + PAIRS), 0.0)
        if nk % 2:
            memset("m_tb%d" % S, V("tt", tb + PAIRS + 16 * (nk - 2), tb + PAIRS + 16 * nk), 0.0)
    memset("m_db", V("db", 31, 32), 0.0)
    memset("m_xx", V("xx", 240, 248), 0.0)
    memset("m_ms", V("ms", 0, 4), 0.0)
    for t in range(R):
        memset("m_dv%d" % t, V("dv%d" % t, 0, PAD), 0.0)

    quant("qu", "uq", "us", 0, 128, V("ub", 0, 512))
    UP = V("upu", 0, 16)
    vec("pkq", lambda: g.vector.tensor_copy(T.u2q[:, 0:256].bitcast(dt.uint32),
                                            T.uq[:, 0:128].bitcast(dt.uint32).indirect(ap(UP))),
        ("gv", 256), [V("uq", 0, 128), UP], [V("u2q", 0, 256)])
    gather("pks", V("u2s", 0, 256), V("us", 0, 128), UP, "va")

    copy("stf", V("stf", 0, 2), V("sti", 0, 2))
    lin("stg", V("stf", 2, 4), V("stf", 0, 2), 1.0, GL)
    for t in range(R):
        lin("bi%d" % t, V("bi", 32 * t, 32 * t + 32), V("xf", 0, 32), 0.0, V("stf", 2 + t, 3 + t))
    transpose("b2", V("b2", 0, 64), V("bi", 0, 64))
    for t in range(R):
        for h in range(2):
            lin("b3%d%d" % (t, h), V("b3", 2 * t + h, 64, 4), V("b2", 32 * t + 16 * h, 32 * t + 16 * h + 16), 1.0, PI)
    gather("bo", V("bo", 0, 32), V("b3", 0, 64), V("lu", 8, 10))
    ts("bo2", V("bo", 32, 64), V("bo", 0, 32), SK, ALU.add, H128, ALU.subtract)
    for side in range(2):
        at = 120 * side
        for k0, nk in RUNS:
            for e in range(2):
                a = 4 * (k0 - 1 + side)
                lin("xx%d_%d_%d" % (side, k0, e), V("xx", at, at + 4 * nk), V("b3", a, a + 4 * nk), 1.0, 4.0 * e)
                at += 4 * nk
    for side in range(2):
        gather("ot%d" % side, V("ot", 64 * side, 64 * side + 64), V("xx", 120 * side, 120 * side + 128),
               V("lu", 4 * side, 4 * side + 4))
    tt("db1", V("db", 0, 31), V("bo", 0, 31), V("bo", 1, 32), ALU.subtract)
    lin("db", V("db", 0, 31), V("db", 0, 31), 1.0, PI)

    def unpack(tag, t, banks, a, b, keep, end):
        at = keep
        for h in range(2):
            k = banks[h]
            mm("ms%s%d%d" % (tag, t, h), k, "u2q", "u2s", 128 * h, "xq%d" % t, "xs%d" % t, a, b)
        for h in range(2):
            k = banks[h]
            scale("cs%s%d%d" % (tag, t, h), V("w2%d" % t, L * h + at, L * h + at + end - keep),
                  V("ps", 512 * k + keep - a, 512 * k + end - a), 1.0)
        for h in range(4):
            k = banks[2 + h]
            mm("md%s%d%d" % (tag, t, h), k, "eq", "es", 128 * h, "xq%d" % t, "xs%d" % t, a, b)
            scale("cd%s%d%d" % (tag, t, h), V("dv%d" % t, PAD + L * h + at, PAD + L * h + at + end - keep),
                  V("ps", 512 * k + keep - a, 512 * k + end - a), 0.5)

    for t in range(R):
        n = lambda s: "%s%d" % (s, t)
        gtt(n("kk"), V(n("kk"), 0, 128), V("bo", 32 + 16 * t, 48 + 16 * t), V("lu", 12, 20), V("q4t", 0, 128), ALU.add)
        ts(n("pn0"), V(n("cf"), 0, 4), V(n("kk"), 0, 8, 2), H128, ALU.add, float(PAD), ALU.subtract)
        lin(n("po0"), V(n("cf"), 4, 8), V(n("kk"), 0, 8, 2), 1.0, H128)
        copy(n("of0"), V(n("off"), 0, 8), V(n("cf"), 0, 8))
        scale(n("pp0"), V(n("po"), 0, 1), V(n("cf"), 4, 5), 1.0)
        gtt(n("pen"), V(n("pen"), 0, 240), V("db", 16 * t, 16 * t + 16), V("lu", 20, 35), V("ci", 0, 240), ALU.is_equal)

    unpack("o", 0, (0, 1, 2, 3, 4, 5), 0, C, 0, C)
    unpack("r", 0, (6, 7, 0, 1, 2, 3), L - 128, L, C, L)
    dma("ldv", "s", lambda: T.vb[:], lambda: T.v[:], 2200, [V("xs0", C, L)], [V("vb", 0, 512)], ["ldwc"])
    quant("qv", "vq", "vs", 0, 128, V("vb", 0, 512))
    for t in range(R):
        n = lambda s: "%s%d" % (s, t)
        state = V("lu", 10, 11)
        scale(n("pes"), V("a0", 1, 960, 4), V(n("pen"), 0, 240), PEN)
        for S, (k0, nk) in enumerate(RUNS):
            m = lambda s: "%s%s%d" % (s, "ABCDEF"[S], t)
            a, c, w, f = 64 * (k0 - 1), 16 * (k0 - 1), 16 * nk, 32 * t + 2 * (k0 - 1)
            for j in range(2):
                x, y = a + 2 * w * j, a + 2 * w * (j + 1)
                gather(m("tg%d" % j), V(n("tg"), x, y), V(n("w2"), 16 + 8 * j, 2 * L), V("ot", f, f + 2 * nk), "va")
                transpose(m("tb%d" % j), V(n("tb"), x, y), V(n("tg"), x, y))
                gtt(m("dd%d" % j), V(n("dd"), x, y), V(n("w2"), 8 * j, 2 * L), V("ot", 64 + f, 64 + f + 2 * nk),
                    V(n("tb"), x, y), ALU.subtract)
            for e in range(4):
                o, i = V(n("ab"), a + e, a + 4 * w, 4), V(n("dd"), a + w * e, a + w * e + w)
                op(m("ab%d" % e), {"a": (lambda o=o, i=i: g.scalar.activation(ap(o), ap(i), ACT.Abs), ("n", w))}, [i], [o])
            scan(m("ms"), V("ms", a + 4, a + 4 * w + 4), V("a0", a, a + 4 * w), V(n("ab"), a, a + 4 * w), ALU.add, ALU.max)
            scan(m("mb"), V(n("mb"), c, c + w), V("ms", a + 3, a + 4 * w, 4), V("rt", 0, w), ALU.min, ALU.max)
            tt(m("nf"), V(n("nf"), c, c + w), V("ms", a + 7, a + 4 * w + 4, 4), V(n("mb"), c, c + w), ALU.is_ge)
            scan(m("cn"), V(n("cn"), c, c + w), V(n("nf"), c, c + w), V("d1", c, c + w), ALU.mult, ALU.add)
            copy(m("fu"), V(n("fu"), 8 * S, 8 * S + nk), V(n("cn"), c + 15, c + w, 16))
            tb, ng = 2 * PAIRS * S, nk - 1 - nk % 2
            gather(m("ft"), V("tt", tb, tb + w), V("idt", 0, 144), V(n("fu"), 8 * S, 8 * S + nk), "va")
            gather(m("gg"), V("tt", tb + PAIRS, tb + PAIRS + 16 * ng), V("tt", tb, tb + w), V(n("fu"), 8 * S, 8 * S + ng), "va")
            table = V("tt", tb, tb + PAIRS + 16 * (ng + 2 * (nk % 2)))
            for k in range(k0, k0 + nk, 2):
                if k in DIRECT:
                    gtt(n("po%d_" % k), V(n("po"), 8 * k, 8 * k + 16), table, state, V(n("kk"), 8 * k, 8 * k + 16), ALU.add)
                else:
                    gather(n("cg%d_" % k), V(n("cg"), 8 * k, 8 * k + 16), table, state, "a")
                if k + 2 < 16:
                    gather(n("st%d_" % k), V(n("sx"), 16 * k, 16 * k + 16), table, state)
                    state = V(n("sx"), 16 * k + (8 if k + 1 < k0 + nk else 0), 16 * k + (9 if k + 1 < k0 + nk else 1))
        for lo, hi in PLACES[t]:
            if lo not in DIRECT:
                tt(n("pt%d_" % lo), V(n("po"), 8 * lo, 8 * hi, 2), V(n("cg"), 8 * lo, 8 * hi, 2), V(n("kk"), 8 * lo, 8 * hi, 2), ALU.add)
            copy(n("off%d_" % lo), V(n("off"), 4 * lo + 4, 4 * hi + 4), V(n("po"), 8 * lo, 8 * hi, 2))
        for lo, hi in TEMPLATES[t]:
            gather(n("nn%d_" % lo), V(n("nn"), 64 * lo, 64 * hi), V(n("dv"), 16, PAD + 4 * L), V(n("off"), 4 * lo, 4 * hi), "va")
        lin(n("pos"), V("pos", 16 * t, 16 * t + 16), V(n("po"), 0, 128, 8), 1.0, -float(PAD))
        if t == 1:
            arrive("aw1", "warr1", peers["from_w1"], [V("wq1", 0, 512), V("wp1", 0, 512)], "swfs")
        nq, ns = "xq%d" % (t + 1), "xs%d" % (t + 1)
        for S, (c, d) in enumerate(((0, CUT[t]), (CUT[t], C))):
            m = lambda s: "%s%s%d" % (s, "AB"[S], t)
            a, z = (0, max(d, 128)) if S == 0 else (min(c, C - 128), C)
            if z > d:
                for name in ("zt", "ht", "xt"):
                    memset(m("m_" + name), V(n(name), 4 * d, 4 * z), 0.0)
            for lo, hi in SUMS[t]:
                if c <= 16 * lo < d:
                    gtt(n("zt%d_" % lo), V(n("zt"), 64 * lo, 64 * hi), V(n("dv"), 0, PAD + 4 * L),
                        V(n("off"), 4 * lo + 4, 4 * hi + 4), V(n("nn"), 64 * lo, 64 * hi), ALU.add)
            quant(m("qz"), n("zq"), n("zs"), a, z, V(n("zt"), 4 * a, 4 * z))
            for b in range(4):
                k = 4 * S + b
                mm(m("mr%d" % b), k, n("wq"), n("wp"), 128 * b, n("zq"), n("zs"), a, z)
                scale(m("ch%d" % b), V(n("ht"), 4 * c + b, 4 * d, 4), V("ps", 512 * k + c - a, 512 * k + d - a), 0.03125)
            quant(m("qh"), n("hq"), n("hs"), a, z, V(n("ht"), 4 * a, 4 * z))
            for b in range(4):
                k = 4 * S + b
                mm(m("mz%d" % b), k, "eq", "es", 128 * b, n("zq"), n("zs"), a, z, True, False)
                mm(m("mh%d" % b), k, "eq", "es", 128 * b, n("hq"), n("hs"), a, z, False, True, m("mz%d" % b))
                scale(m("cx%d" % b), V(n("xt"), 4 * c + b, 4 * d, 4), V("ps", 512 * k + c - a, 512 * k + d - a), 1.0)
            quant(m("qx"), nq, ns, a, z, V(n("xt"), 4 * a, 4 * z))
            if t == 0 and S == 0:
                ship("sx1", peers["prev"], "xarr1", "xq1", "xs1", C, "xq1", "xs1", 0, B)
                ship("swf", peers["prev"] if peers["forward"] else None, "warr1", "wq1", "wp1", 0, "wq0", "wp0", 0, 512)
                arrive("ax1", "xarr1", peers["from_next"], [V("xq1", C, L), V("xs1", C, L)], "sx1s")
                unpack("a", 1, (0, 1, 2, 3, 0, 1), a, z, c, d)
            if t == 0 and S == 1:
                unpack("b", 1, (0, 1, 2, 3, 4, 5), c, L, c, L)
            if t == 1:
                mm(m("my"), 4 * S, "vq", "vs", 0, nq, ns, a, z)
                scale(m("cy"), V("yb", c, d), V("ps", 2048 * S + c - a, 2048 * S + d - a), 1.0)

    dma("ool", "s", lambda: T.ol[:], lambda: T.pos[0:128:16, :], 1, [V("pos", 0, 32)], [])
    cut = min(CUT[1], C - 128)
    for S, (c, d, e, f) in enumerate(((0, cut, 0, CUT[1]), (cut, C, CUT[1], C))):
        dma("ooc%d" % S, "sa", lambda c=c, d=d: T.oc[:, 4 * c:4 * d],
            lambda c=c, d=d: T.xq2[:, c:d].bitcast(dt.uint8), (d - c) / 2, [V("xq2", c, d)], [])
        dma("oy%d" % S, "sa", lambda e=e, f=f: T.y[:, e:f], lambda e=e, f=f: T.yb[:, e:f], (f - e) / 2, [V("yb", e, f)], [])
    for k in range(4):
        dma("osc%d" % k, "sa", lambda k=k: T.osc[4 * k:4 * k + 4, :], lambda k=k: T.xs2[32 * k:32 * k + 4, 0:C], 1,
            [V("xs2", 0, C)], [])
    return ops


def depend(ops):
    index = {o["name"]: i for i, o in enumerate(ops)}
    seen = {}
    for i, o in enumerate(ops):
        dep = set()
        acc = index[o["acc"]] if o["acc"] else None
        for views, writes in ((o["rd"], False), (o["wr"], True)):
            for v in views:
                m = span(v)
                for (m2, j, w2) in seen.get(v[0], []):
                    if m & m2 and (writes or w2) and j != acc and j != i:
                        dep.add(j)
        for views, writes in ((o["rd"], False), (o["wr"], True)):
            for v in views:
                m = span(v)
                old = seen.get(v[0], [])
                if writes:
                    old = [e for e in old if e[0] & ~m]
                seen[v[0]] = old + [(m, i, writes)]
        o["dep"] = dep
        o["aft"] = set(index[a] for a in o["after"]) | (set() if acc is None else {acc})
    return index


PLAN = {"cycle": 1.04, "gather": 1.62, "tensor": 0.7, "scalar": 15.0, "hand": 105.0, "dma": 1800.0, "kb": 5.0, "remote": 3100.0,
        "first": 500.0, "layer": 4500.0, "seed": 1, "turns": 40000, "allow": 100.0, "early": 1.0, "reach": 800.0}


def times(cost, first, q):
    kind, n = cost
    if kind == "dma":
        return 60.0, PLAN["dma"] + PLAN["kb"] * n
    if kind == "rem":
        return 300.0 + (PLAN["first"] if first else 0.0), 0.0
    if kind == "arr":
        return 0.0, PLAN["remote"] + n
    t = {"n": PLAN["cycle"] * (max(64, n) if q == "v" else PLAN["scalar"] + n), "gv": 62 + PLAN["gather"] * n, "ga": 81 + PLAN["gather"] * n,
         "q": 15 + 0.275 * n, "mm": PLAN["tensor"] * (n + 16), "io": 160 + 2 * PLAN["cycle"] * n}[kind]
    return t, t


def plan(ops):
    n = len(ops)
    first = [i for i in range(n) if ops[i]["kind"] in ("rem", "none")][0]
    tm = [{q: times(a[1], i == first, q) for q, a in o["alts"].items()} for i, o in enumerate(ops)]
    users = [[] for _ in ops]
    for i, o in enumerate(ops):
        for d in o["dep"] | o["aft"]:
            users[d].append(i)
    rank = [None] * n

    def way(i):
        if rank[i] is None:
            rank[i] = max(min(tm[i].values())) + max([way(u) + PLAN["hand"] for u in users[i]] + [0.0])
        return rank[i]

    for i in reversed(range(n)):
        way(i)
    hand = PLAN["hand"]
    dep, aft = [list(o["dep"]) for o in ops], [list(o["aft"]) for o in ops]
    needs = [dep[i] + aft[i] for i in range(n)]
    either = ["v" in tm[i] and "a" in tm[i] for i in range(n)]

    def place(prio, force):
        starts, ends = {q: [] for q in "vapsgx"}, {q: [] for q in "vapsgx"}
        at, fin, end, queue = [0.0] * n, [0.0] * n, [0.0] * n, [None] * n
        for i in sorted(range(n), key=lambda i: -prio[i]):
            r = max([fin[d] + hand for d in dep[i]] + [end[d] for d in aft[i]] + [0.0])
            best = None
            for q, (hold, lat) in tm[i].items():
                if force[i] in (None, q):
                    s, a, b = r, starts[q], ends[q]
                    k = len(b)
                    while k and b[k - 1] > s:
                        k -= 1
                    while k < len(a) and s + hold > a[k]:
                        s = max(s, b[k])
                        k += 1
                    if best is None or s + lat < best[0]:
                        best = (s + lat, s, q, k)
            fin[i], at[i], q, k = best
            end[i], queue[i] = at[i] + tm[i][q][0], q
            if q != "x":
                starts[q].insert(k, at[i])
                ends[q].insert(k, end[i])
        return max(fin), at, fin, end, queue

    def tight(p):
        total, at, fin, end, queue = p
        ahead = {(queue[i], end[i]): i for i in range(n)}
        i, calls, pairs = fin.index(total), [], []
        while i is not None:
            calls.append(i)
            c = [d for d in dep[i] if fin[d] + hand == at[i]] + [d for d in aft[i] if end[d] == at[i]]
            before = c[0] if c else ahead.get((queue[i], at[i]))
            if before is not None and not c:
                pairs.append((before, i))
            i = before
        return calls, pairs

    def move(prio, i, to):
        up = to > prio[i]
        prio[i], todo = to, [i]
        while todo:
            x = todo.pop()
            for d in (needs[x] if up else users[x]):
                if (prio[d] <= prio[x]) if up else (prio[d] >= prio[x]):
                    prio[d] = prio[x] + (0.001 if up else -0.001)
                    todo.append(d)

    seed = [PLAN["seed"]]

    def draw():
        seed[0] = (seed[0] * 6364136223846793005 + 1442695040888963407) % 2 ** 64
        return (seed[0] >> 11) / 2.0 ** 53

    def worth(p):
        return p[0] + PLAN["early"] * sum(p[1]) / n

    now = best = place(rank, [None] * n)
    calls, pairs = tight(now)
    for turn in range(PLAN["turns"]):
        p, f, r = [-now[1][i] - 0.0001 * i for i in range(n)], list(now[4]), draw()
        if r < 0.6 and pairs:
            u, v = pairs[int(draw() * len(pairs))]
            x = u if draw() < 0.5 else v
            if r < 0.18 and either[x]:
                f[x] = "a" if f[x] == "v" else "v"
            elif x == v:
                move(p, v, p[u] + 1 + PLAN["reach"] * draw() ** 2)
            else:
                move(p, u, p[v] - 1 - 2 * PLAN["reach"] * draw() ** 2)
        elif r < 0.75:
            x = calls[int(draw() * len(calls))]
            move(p, x, p[x] + PLAN["reach"] * draw())
        else:
            x = int(draw() * n)
            if r < 0.85 and either[x]:
                f[x] = "a" if f[x] == "v" else "v"
            else:
                move(p, x, p[x] + 2 * PLAN["reach"] * (draw() - draw()))
        e = place(p, f)
        if worth(e) <= worth(now) - PLAN["allow"] * math.log(1 - draw()) * (1 - turn / PLAN["turns"]):
            now = e
            calls, pairs = tight(now)
            if worth(e) < worth(best):
                best = e
    PLANNED.append(best)
    return [(i, best[4][i]) for i in sorted(range(n), key=lambda i: (best[1][i], i)) if best[4][i] != "x"]


PLANNED, ORDER = [], []


def emit(g, T, ops, order):
    queues = {"v": g.vector, "a": g.scalar, "p": g.tensor, "s": g.sync, "g": g}
    known = {q: set() for q in queues}
    closure, waits, before, needed = {}, {}, {}, set()
    for i, o in enumerate(ops):
        if o["kind"] == "ext":
            closure[i] = {i}
    for i, q in order:
        need = [d for d in ops[i]["dep"] if d not in known[q]]
        need = sorted(d for d in need if not any(e != d and d in closure[e] for e in need))
        waits[i] = need
        for d in need:
            known[q] |= closure[d]
            needed.add(d)
        before[i] = set(known[q])
        closure[i] = before[i] | {i}
    stores = [i for i, q in order if ops[i]["kind"] == "dma" and not ops[i]["wr"]]
    needed |= set(stores)
    last, count, mark = [None] * NPOOL, [0] * NPOOL, {}
    for i, o in enumerate(ops):
        if o["kind"] == "ext":
            mark[i] = o["ext"]
    sent = 0
    for i, q in order:
        for d in waits[i]:
            queues[q].wait_ge(T.sem[mark[d][0]], mark[d][1])
        ins = ops[i]["alts"][q][0]()
        sent += ops[i].get("eng", 0)
        if i in needed:
            s = [k for k in range(NPOOL) if last[k] is None or last[k] in before[i]][0]
            step = 16 if ops[i]["kind"] == "dma" else 1
            last[s] = i
            count[s] += step
            mark[i] = ("s%d" % s, count[s])
            ins.then_inc(T.sem["s%d" % s], step)
    for i in stores:
        g.sync.wait_ge(T.sem[mark[i][0]], mark[i][1])
    g.wait_ge(T.sem["sent"], sent)


def wiring(T, topo, rank):
    cores, n = T.cores, len(T.cores)

    def engines(a, b):
        e = topo.engines(cores[a % n], cores[b % n])
        return e[len(e) // 2:] if together(a, b) else e

    def together(a, b):
        return topo.chip(cores[a % n]) == topo.chip(cores[b % n])

    def peer(b):
        e = engines(rank, b)
        rid, pid = topo.addr(cores[b % n])[:2]
        return (rid, pid, sum(1 << k for k in e), len(e))

    def relayed(q):
        return together(q, q + 1) and not together(q, q + 2)

    def helped(q):
        return relayed(q) and not together(q, q - 1)

    return {"prev": peer(rank - 1), "direct": None if relayed(rank - 2) else peer(rank - 2), "forward": relayed(rank - 1),
            "helper": peer(rank + 1) if helped(rank) else None,
            "from_next": 2 * len(engines(rank + 1, rank)), "from_prev": 2 * len(engines(rank - 1, rank)),
            "from_w0": 2 * len(engines(rank + 1, rank)) + (2 * len(engines(rank + 2, rank)) if helped(rank + 1) else 0),
            "from_w1": 2 * len(engines(rank + (1 if relayed(rank) else 2), rank))}


def rank_program(g, core, T, topo):
    rank = T.rank_of(core)
    if rank is None:
        return
    ops = program(g, T, wiring(T, topo, rank))
    depend(ops)
    if not ORDER:
        ORDER.extend(plan(ops))
    emit(g, T, ops, [e for e in ORDER if ops[e[0]]["kind"] != "none"])
